import numpy as np
import ml_dtypes


def mxq(x, axis, fmt="e4m3"):
    dtype, down = {"e4m3": (ml_dtypes.float8_e4m3fn, 7), "e5m2": (ml_dtypes.float8_e5m2, 14)}[fmt]
    v = np.moveaxis(np.asarray(x, np.float32).astype(ml_dtypes.bfloat16).astype(np.float64), axis, -1)
    blocks = v.reshape(v.shape[:-1] + (-1, 32))
    amax = np.abs(blocks).max(-1, keepdims=True)
    byte = np.maximum(np.where(amax > 0, np.frexp(amax)[1] - 1 + 127, 0) - down, 1)
    scale = np.exp2(byte - 127.0)
    codes = (blocks / scale).astype(np.float32).astype(dtype).astype(np.float64)
    return np.moveaxis((codes * scale).reshape(v.shape), -1, axis)


WIDE = False


def mx_kscale(k):
    if not WIDE:
        return np.ones(k)
    levels = np.array([10, -10, 5, -5, 0])
    if k % 512:
        return np.exp2(np.random.permutation(np.resize(levels, k // 32))).repeat(32)
    a = np.empty((k // 512, 16))
    for p in range(k // 512):
        a[p, :8] = np.random.permutation(np.resize(levels, 8))
        for g in range(8):
            far = levels[np.abs(levels - a[p, g]) >= 10]
            a[p, g + 8] = far[np.random.randint(len(far))]
    return np.exp2(a.ravel()).repeat(32)


def f64(x):
    return np.asarray(x).astype(np.float64)


def striped(idx):
    return np.tile(np.asarray(idx).reshape(-1, 16).T, (8, 1)).astype(np.uint16)


def unstriped(offs):
    return offs[:16].T.reshape(-1).astype(np.int64)


E2M1 = np.array([0.0, 0.5, 1.0, 1.5, 2.0, 3.0, 4.0, 6.0, -0.0, -0.5, -1.0, -1.5, -2.0, -3.0, -4.0, -6.0])


def pack_weight(w, fmt):
    k, n = w.shape
    w = f64(np.asarray(w, np.float32).astype(ml_dtypes.bfloat16)).reshape(k // 32, 32, n)
    amax = np.abs(w).max(1)
    if fmt == "e4m3":
        byte = np.frexp(amax)[1] - 1 + 127 - 7
    else:
        mant, ex = np.frexp(amax / 6.0)
        byte = np.where(mant > 0.5, ex, ex - 1) + 127
    byte = np.clip(np.where(amax > 0, byte, 1), 1, 254)
    scaled = (w * np.exp2(127.0 - byte)[:, None, :]).reshape(k, n).astype(np.float32)
    by_word = np.ascontiguousarray(scaled.reshape(k // 512, 128, 4, n).transpose(0, 1, 3, 2))
    if fmt == "e4m3":
        words = by_word.astype(ml_dtypes.float8_e4m3fn).view(np.uint8)
    else:
        c = by_word.astype(ml_dtypes.float4_e2m1fn).view(np.uint8) & 0xF
        words = (c[..., 0::2] | (c[..., 1::2] << 4)).reshape(k // 512, 128, 2 * n)
    return np.ascontiguousarray(words), np.ascontiguousarray(byte.astype(np.uint8).reshape(k // 512, 16, n))


def unpack_weight(words, scales, fmt):
    g, _, n = scales.shape
    words = np.ascontiguousarray(words).reshape(g, 128, n, -1)
    if fmt == "e4m3":
        vals = words.view(ml_dtypes.float8_e4m3fn).astype(np.float64)
    else:
        nib = np.empty((g, 128, n, 4), np.uint8)
        nib[..., 0::2] = words & 0xF
        nib[..., 1::2] = words >> 4
        vals = E2M1[nib]
    vals = vals * np.repeat(np.exp2(scales.astype(np.float64) - 127.0), 8, axis=1)[..., None]
    return vals.transpose(0, 1, 3, 2).reshape(g * 512, n)


D, T, I, Q, E = 512, 2048, 512, 256, 512


def setup_inputs():
    n = np.random.standard_normal
    idx = np.random.permutation(T)[:I]
    fd = mx_kscale(D)
    fi = mx_kscale(I)
    ti = np.ones(T)
    ti[idx] = fi
    keysp = pack_weight(n((D, T)) / fd[:, None], "e4m3")
    return {
        "query": (n((D, Q)) * 0.4 / np.sqrt(D) * fd[:, None]).astype(np.float32),
        "keys_words": keysp[0],
        "keys_scales": keysp[1],
        "fac": (np.random.uniform(0.5, 2.0, (I, 1)) * fi[:, None]).astype(np.float32),
        "vals": (n((E, T)) / ti).astype(np.float32),
        "offs": striped(idx),
    }


def reference(query, keys_words, keys_scales, fac, vals, offs):
    idx = unstriped(offs)
    keysu = unpack_weight(keys_words, keys_scales, "e4m3")
    queryq = mxq(f64(query), 0, "e4m3")
    keysidxg = keysu[:, idx]
    a = queryq.T @ keysidxg
    p = np.exp(a)
    r = p / np.sum(p, axis=1, keepdims=True)
    rt = r.T
    w = rt * f64(fac) / np.sum(rt, axis=1, keepdims=True)
    vt = f64(vals)[:, idx].T
    wq = mxq(w, 0, "e4m3")
    vtq = mxq(vt, 0, "e4m3")
    o = wq.T @ vtq
    return o

@@ -1,0 +1,179 @@
+from contextlib import ExitStack
+
+import concourse.mybir as mybir
+from concourse.masks import make_identity
+
+D, T, I, Q, E = 512, 2048, 512, 256, 512
+FLOPS = 2 * Q * D * I + 2 * Q * I * E
+
+F32 = mybir.dt.float32
+BF16 = mybir.dt.bfloat16
+I32 = mybir.dt.int32
+U32 = mybir.dt.uint32
+U16 = mybir.dt.uint16
+U8 = mybir.dt.uint8
+FP8X4 = mybir.dt.float8_e4m3fn_x4
+ALU = mybir.AluOpType
+ACT = mybir.ActivationFunctionType
+AXIS_X = mybir.AxisListType.X
+
+P = 128
+PACK = 4
+HALVES = Q // P
+BLOCKS = E // P
+
+
+def tile_attend_sinkhorn_kernel(tc, query, keys_words, keys_scales, fac, vals, offs, out):
+    nc = tc.nc
+    with ExitStack() as ctx:
+        keep = ctx.enter_context(tc.tile_pool(name="keep", bufs=1))
+        psum = ctx.enter_context(tc.psum_pool(name="psum", bufs=1))
+
+        def sbuf(shape, dtype, name, tag=None):
+            return keep.tile(shape, dtype, name=name, tag=tag or name, align_bytes=64)
+
+        offsets = keep.tile([P, I // 16], U16, name="offsets")
+        nc.sync.dma_start(offsets[:], offs)
+
+        key_words = sbuf([P, T], U32, "key_words")
+        nc.sync.dma_start(key_words[:].bitcast(I32), keys_words[0].rearrange("p n t -> p (n t)").bitcast(I32))
+
+        key_scales = sbuf([P, T], U8, "key_scales")
+        nc.vector.memset(key_scales[:].bitcast(I32), 0)
+        for quad in range(4):
+            nc.scalar.dma_start(
+                key_scales[32 * quad : 32 * quad + 4, :].bitcast(I32),
+                keys_scales[0, 4 * quad : 4 * quad + 4, :].bitcast(I32),
+            )
+
+        warm = sbuf([P, 1], F32, "warm")
+        warm_out = sbuf([P, 1], F32, "warm_out")
+        nc.vector.memset(warm[:], 0.0)
+        nc.scalar.activation(warm_out[:], warm[:], ACT.Exp)
+
+        query_rows = query.rearrange("(p j) q -> p j q", j=PACK)
+        query_raw = []
+        for h in range(HALVES):
+            raw = sbuf([P, PACK, P], F32, f"query_raw{h}")
+            nc.sync.dma_start(raw[:], query_rows[:, :, h * P : (h + 1) * P])
+            query_raw.append(raw)
+
+        ident = sbuf([P, P], F32, "ident")
+        make_identity(nc, ident[:])
+
+        got_scales = sbuf([P, I], U8, "got_scales")
+        nc.vector.tensor_copy(got_scales[:], key_scales[:].indirect(offsets[:]))
+        got_words = sbuf([P, I], U32, "got_words", tag="key_scales")
+        nc.vector.tensor_copy(got_words[:], key_words[:].indirect(offsets[:]))
+
+        scores = []
+        for h in range(HALVES):
+            query_bf = sbuf([P, P, PACK], BF16, f"query_bf{h}")
+            nc.scalar.copy(
+                query_bf[:].rearrange("p (c i) j -> p c j i", i=4),
+                query_raw[h][:].rearrange("p j (c i) -> p c j i", i=4),
+            )
+            q_codes = sbuf([P, P], U32, f"q_codes{h}")
+            q_scales = sbuf([P, P], U8, f"q_scales{h}")
+            nc.vector.quantize_mx(q_codes[:].bitcast(FP8X4), q_scales[:], query_bf[:].rearrange("p q j -> p (q j)"))
+            score = psum.tile([P, I], F32, name=f"score{h}", tag=f"score{h}")
+            nc.tensor.matmul_mx(
+                score[:], lhsT=q_codes[:].bitcast(FP8X4), lhsT_scale=q_scales[:],
+                rhs=got_words[:].bitcast(FP8X4), rhs_scale=got_scales[:], start=True, stop=True,
+            )
+            scores.append(score)
+
+        pools = []
+        for c, held_by in enumerate(("warm", "query_raw0", "query_raw1", "query_bf0")):
+            pool = sbuf([P, T], F32, f"vals{c}", tag=held_by)
+            nc.sync.dma_start(pool[:], vals[c * P : (c + 1) * P, :])
+            pools.append(pool)
+            if c == 0:
+                fac_sb = sbuf([P, PACK], F32, "fac_sb", tag="warm_out")
+                nc.sync.dma_start(fac_sb[:], fac.rearrange("(p t) o -> p (t o)", t=PACK))
+
+        def gather_values(c, held_by):
+            got = sbuf([P, I], BF16, f"got_vals{c}", tag=held_by)
+            nc.vector.tensor_copy(got[:], pools[c][:].indirect(offsets[:]))
+            return got
+
+        def quantize_values(c, got):
+            pairs = got[:].bitcast(F32)
+            v_turned = psum.tile([P, 2, P], F32, name=f"v_turned{c % 2}", tag=f"v_turned{c % 2}")
+            for u in range(2):
+                nc.tensor.transpose(v_turned[:, u, :], pairs[:, u : I // 2 : 2], ident[:])
+            v_bf = sbuf([P, P * PACK], BF16, f"v_bf{c}")
+            nc.scalar.copy(
+                v_bf[:].bitcast(F32).rearrange("p (e u) -> p e u", u=2), v_turned[:].rearrange("p u e -> p e u")
+            )
+            v_codes = sbuf([P, P], U32, f"v_codes{c}")
+            v_scales = sbuf([P, P], U8, f"v_scales{c}")
+            nc.vector.quantize_mx(v_codes[:].bitcast(FP8X4), v_scales[:], v_bf[:])
+            return v_codes, v_scales
+
+        row_sum = sbuf([P, HALVES], F32, "row_sum")
+        expds = []
+        for h in range(HALVES):
+            neg_max = sbuf([P, 1], F32, f"neg_max{h}")
+            nc.vector.tensor_reduce(neg_max[:], scores[h][:], AXIS_X, ALU.max, negate=True)
+            expd = sbuf([P, PACK, P], F32, f"expd{h}")
+            nc.scalar.activation(
+                expd[:], scores[h][:].rearrange("p (s t) -> p t s", t=PACK), ACT.Exp,
+                bias=neg_max[:], accum_out=row_sum[:, h : h + 1],
+            )
+            expds.append(expd)
+        gots = [gather_values(0, "q_codes1")]
+        row_inv = sbuf([P, HALVES], F32, "row_inv")
+        nc.vector.reciprocal(row_inv[:], row_sum[:])
+        rows = [sbuf([P, PACK, P], F32, f"row{h}") for h in range(HALVES)]
+        nc.scalar.activation(rows[0][:], expds[0][:], ACT.Copy, scale=row_inv[:, 0:1])
+        nc.vector.tensor_scalar(rows[1][:], expds[1][:], row_inv[:, 1:2], None, ALU.mult)
+        gots.append(gather_values(1, "expd1"))
+
+        both = psum.tile([P, PACK, P], F32, name="both")
+        turned = [psum.tile([P, PACK, P], F32, name=f"turned{h}") for h in range(HALVES)]
+        for n, h in enumerate((1, 0)):
+            for t in range(PACK):
+                nc.tensor.matmul(
+                    both[:, t, :], lhsT=rows[h][:, t, :], rhs=ident[:], is_transpose=True,
+                    start=(n == 0 and t == 0), stop=(n == HALVES - 1 and t == PACK - 1),
+                )
+        for h in range(HALVES):
+            for t in range(PACK):
+                nc.tensor.transpose(turned[h][:, t, :], rows[h][:, t, :], ident[:])
+
+        col_sum = sbuf([P, PACK], F32, "col_sum")
+        nc.vector.tensor_reduce(col_sum[:], both[:], AXIS_X, ALU.add)
+        col_inv = sbuf([P, PACK], F32, "col_inv")
+        nc.vector.reciprocal(col_inv[:], col_sum[:])
+        gain = sbuf([P, PACK], F32, "gain")
+        nc.vector.tensor_tensor(gain[:], col_inv[:], fac_sb[:], ALU.mult)
+
+        w_bf = sbuf([P, HALVES, P, PACK], BF16, "w_bf")
+        w_codes = sbuf([P, Q], U32, "w_codes")
+        w_scales = sbuf([P, Q], U8, "w_scales")
+        for h in range(HALVES):
+            nc.vector.tensor_tensor(
+                w_bf[:, h], turned[h][:].rearrange("p t q -> p q t"),
+                gain[:].unsqueeze(1).to_broadcast([P, P, PACK]), ALU.mult,
+            )
+        quantized = [quantize_values(c, gots[c]) for c in range(2)]
+        nc.vector.quantize_mx(w_codes[:].bitcast(FP8X4), w_scales[:], w_bf[:].rearrange("p h q t -> p (h q t)"))
+
+        gots.append(gather_values(2, "gain"))
+        gots.append(gather_values(3, "w_bf"))
+        quantized.extend(quantize_values(c, gots[c]) for c in range(2, BLOCKS))
+
+        out_rows = out.rearrange("(h p) e -> p h e", p=P)
+        for c in range(BLOCKS):
+            v_codes, v_scales = quantized[c]
+            acc = psum.tile([P, HALVES, P], F32, name=f"acc{c}", tag=f"score{c % 2}")
+            for h in range(HALVES):
+                nc.tensor.matmul_mx(
+                    acc[:, h, :], lhsT=w_codes[:, h * P : (h + 1) * P].bitcast(FP8X4),
+                    lhsT_scale=w_scales[:, h * P : (h + 1) * P],
+                    rhs=v_codes[:].bitcast(FP8X4), rhs_scale=v_scales[:], start=True, stop=True,
+                )
+            result = sbuf([P, HALVES, P], F32, f"result{c}")
+            nc.scalar.copy(result[:], acc[:])
+            nc.sync.dma_start(out_rows[:, :, c * P : (c + 1) * P], result[:])

@@ -21,6 +21,7 @@ P = 128
 PACK = 4
 HALVES = Q // P
 BLOCKS = E // P
+LOAD_ORDER = (0, 2, 1, 3)
 
 
 def tile_attend_sinkhorn_kernel(tc, query, keys_words, keys_scales, fac, vals, offs, out):
@@ -35,35 +36,38 @@ def tile_attend_sinkhorn_kernel(tc, query, keys_words, keys_scales, fac, vals, o
         offsets = keep.tile([P, I // 16], U16, name="offsets")
         nc.sync.dma_start(offsets[:], offs)
 
-        key_words = sbuf([P, T], U32, "key_words")
-        nc.sync.dma_start(key_words[:].bitcast(I32), keys_words[0].rearrange("p n t -> p (n t)").bitcast(I32))
+        query_rows = query.rearrange("(p j) q -> p j q", j=PACK)
+
+        def load_query(h):
+            raw = sbuf([P, PACK, P], F32, f"query_raw{h}")
+            nc.sync.dma_start(raw[:], query_rows[:, :, h * P : (h + 1) * P])
+            return raw
+
+        query_raw = [load_query(0)]
 
         key_scales = sbuf([P, T], U8, "key_scales")
         nc.vector.memset(key_scales[:].bitcast(I32), 0)
         for quad in range(4):
-            nc.scalar.dma_start(
+            nc.sync.dma_start(
                 key_scales[32 * quad : 32 * quad + 4, :].bitcast(I32),
                 keys_scales[0, 4 * quad : 4 * quad + 4, :].bitcast(I32),
             )
 
+        key_words = sbuf([P, T], U32, "key_words")
+        nc.sync.dma_start(key_words[:].bitcast(I32), keys_words[0].rearrange("p n t -> p (n t)").bitcast(I32))
+        query_raw.append(load_query(1))
+
         warm = sbuf([P, 1], F32, "warm")
         warm_out = sbuf([P, 1], F32, "warm_out")
-        nc.vector.memset(warm[:], 0.0)
+        nc.gpsimd.memset(warm[:], 0.0)
         nc.scalar.activation(warm_out[:], warm[:], ACT.Exp)
-
-        query_rows = query.rearrange("(p j) q -> p j q", j=PACK)
-        query_raw = []
-        for h in range(HALVES):
-            raw = sbuf([P, PACK, P], F32, f"query_raw{h}")
-            nc.sync.dma_start(raw[:], query_rows[:, :, h * P : (h + 1) * P])
-            query_raw.append(raw)
 
         ident = sbuf([P, P], F32, "ident")
         make_identity(nc, ident[:])
 
         got_scales = sbuf([P, I], U8, "got_scales")
         nc.vector.tensor_copy(got_scales[:], key_scales[:].indirect(offsets[:]))
-        got_words = sbuf([P, I], U32, "got_words", tag="key_scales")
+        got_words = sbuf([P, I], U32, "got_words")
         nc.vector.tensor_copy(got_words[:], key_words[:].indirect(offsets[:]))
 
         scores = []
@@ -84,96 +88,124 @@ def tile_attend_sinkhorn_kernel(tc, query, keys_words, keys_scales, fac, vals, o
             scores.append(score)
 
         pools = []
-        for c, held_by in enumerate(("warm", "query_raw0", "query_raw1", "query_bf0")):
-            pool = sbuf([P, T], F32, f"vals{c}", tag=held_by)
-            nc.sync.dma_start(pool[:], vals[c * P : (c + 1) * P, :])
+        for n, block in enumerate(LOAD_ORDER):
+            pool = sbuf([P, T], F32, f"vals{n}")
+            nc.sync.dma_start(pool[:], vals[block * P : (block + 1) * P, :])
             pools.append(pool)
-            if c == 0:
-                fac_sb = sbuf([P, PACK], F32, "fac_sb", tag="warm_out")
+            if n == 1:
+                fac_sb = sbuf([P, PACK], F32, "fac_sb")
                 nc.sync.dma_start(fac_sb[:], fac.rearrange("(p t) o -> p (t o)", t=PACK))
 
-        def gather_values(c, held_by):
-            got = sbuf([P, I], BF16, f"got_vals{c}", tag=held_by)
-            nc.vector.tensor_copy(got[:], pools[c][:].indirect(offsets[:]))
-            return got
-
-        def quantize_values(c, got):
-            pairs = got[:].bitcast(F32)
-            v_turned = psum.tile([P, 2, P], F32, name=f"v_turned{c % 2}", tag=f"v_turned{c % 2}")
-            for u in range(2):
-                nc.tensor.transpose(v_turned[:, u, :], pairs[:, u : I // 2 : 2], ident[:])
-            v_bf = sbuf([P, P * PACK], BF16, f"v_bf{c}")
-            nc.scalar.copy(
-                v_bf[:].bitcast(F32).rearrange("p (e u) -> p e u", u=2), v_turned[:].rearrange("p u e -> p e u")
-            )
-            v_codes = sbuf([P, P], U32, f"v_codes{c}")
-            v_scales = sbuf([P, P], U8, f"v_scales{c}")
-            nc.vector.quantize_mx(v_codes[:].bitcast(FP8X4), v_scales[:], v_bf[:])
-            return v_codes, v_scales
-
-        row_sum = sbuf([P, HALVES], F32, "row_sum")
-        expds = []
+        expds, row_sums = [], []
         for h in range(HALVES):
             neg_max = sbuf([P, 1], F32, f"neg_max{h}")
             nc.vector.tensor_reduce(neg_max[:], scores[h][:], AXIS_X, ALU.max, negate=True)
             expd = sbuf([P, PACK, P], F32, f"expd{h}")
+            row_sum = sbuf([P, 1], F32, f"row_sum{h}")
             nc.scalar.activation(
                 expd[:], scores[h][:].rearrange("p (s t) -> p t s", t=PACK), ACT.Exp,
-                bias=neg_max[:], accum_out=row_sum[:, h : h + 1],
+                bias=neg_max[:], accum_out=row_sum[:],
             )
             expds.append(expd)
-        gots = [gather_values(0, "q_codes1")]
-        row_inv = sbuf([P, HALVES], F32, "row_inv")
-        nc.vector.reciprocal(row_inv[:], row_sum[:])
-        rows = [sbuf([P, PACK, P], F32, f"row{h}") for h in range(HALVES)]
-        nc.scalar.activation(rows[0][:], expds[0][:], ACT.Copy, scale=row_inv[:, 0:1])
-        nc.vector.tensor_scalar(rows[1][:], expds[1][:], row_inv[:, 1:2], None, ALU.mult)
-        gots.append(gather_values(1, "expd1"))
+            row_sums.append(row_sum)
+        rows = []
+        for h in range(HALVES):
+            row_inv = sbuf([P, 1], F32, f"row_inv{h}")
+            nc.vector.reciprocal(row_inv[:], row_sums[h][:])
+            row = sbuf([P, PACK, P], F32, f"row{h}")
+            nc.vector.tensor_scalar(row[:], expds[h][:], row_inv[:], None, ALU.mult)
+            rows.append(row)
 
-        both = psum.tile([P, PACK, P], F32, name="both")
-        turned = [psum.tile([P, PACK, P], F32, name=f"turned{h}") for h in range(HALVES)]
-        for n, h in enumerate((1, 0)):
+        both = [psum.tile([P, 2, P], F32, name=f"both{u}", tag=f"turned{u}") for u in range(2)]
+        for h in range(HALVES):
             for t in range(PACK):
                 nc.tensor.matmul(
-                    both[:, t, :], lhsT=rows[h][:, t, :], rhs=ident[:], is_transpose=True,
-                    start=(n == 0 and t == 0), stop=(n == HALVES - 1 and t == PACK - 1),
+                    both[t // 2][:, t % 2, :], lhsT=rows[h][:, t, :], rhs=ident[:], is_transpose=True,
+                    start=(h == 0 and t % 2 == 0), stop=(h == HALVES - 1 and t % 2 == 1),
                 )
+
+        def gather_values(n, held_by):
+            got = sbuf([P, I], BF16, f"got_vals{n}", tag=held_by)
+            nc.vector.tensor_copy(got[:], pools[n][:].indirect(offsets[:]))
+            return got
+
+        gots = {0: gather_values(0, "expd1"), 2: gather_values(2, "vals0"), 3: gather_values(3, "vals2")}
+
+        vals_bf = sbuf([P, T], BF16, "vals_bf", tag="neg_max1")
+        nc.scalar.activation(vals_bf[:], pools[1][:], ACT.Copy)
+        gots[1] = sbuf([P, I], BF16, "got_vals1")
+        nc.scalar.activation(gots[1][:], vals_bf[:].indirect(offsets[:]), ACT.Copy)
+
+        col_sum = sbuf([P, PACK], F32, "col_sum")
+        summed = sbuf([P, P], BF16, "summed", tag="neg_max1")
+        for t in range(PACK):
+            nc.scalar.activation(summed[:], both[t // 2][:, t % 2, :], ACT.Copy, accum_out=col_sum[:, t : t + 1])
+
+        turned = [psum.tile([P, PACK, P], F32, name=f"turned{h}", tag=f"turned{h}") for h in range(HALVES)]
         for h in range(HALVES):
             for t in range(PACK):
                 nc.tensor.transpose(turned[h][:, t, :], rows[h][:, t, :], ident[:])
 
-        col_sum = sbuf([P, PACK], F32, "col_sum")
-        nc.vector.tensor_reduce(col_sum[:], both[:], AXIS_X, ALU.add)
-        col_inv = sbuf([P, PACK], F32, "col_inv")
+        col_inv = sbuf([P, PACK], F32, "col_inv", tag="vals3")
         nc.vector.reciprocal(col_inv[:], col_sum[:])
         gain = sbuf([P, PACK], F32, "gain")
         nc.vector.tensor_tensor(gain[:], col_inv[:], fac_sb[:], ALU.mult)
 
         w_bf = sbuf([P, HALVES, P, PACK], BF16, "w_bf")
-        w_codes = sbuf([P, Q], U32, "w_codes")
-        w_scales = sbuf([P, Q], U8, "w_scales")
         for h in range(HALVES):
             nc.vector.tensor_tensor(
                 w_bf[:, h], turned[h][:].rearrange("p t q -> p q t"),
                 gain[:].unsqueeze(1).to_broadcast([P, P, PACK]), ALU.mult,
             )
-        quantized = [quantize_values(c, gots[c]) for c in range(2)]
+        w_codes = sbuf([P, Q], U32, "w_codes")
+        w_scales = sbuf([P, Q], U8, "w_scales")
         nc.vector.quantize_mx(w_codes[:].bitcast(FP8X4), w_scales[:], w_bf[:].rearrange("p h q t -> p (h q t)"))
 
-        gots.append(gather_values(2, "gain"))
-        gots.append(gather_values(3, "w_bf"))
-        quantized.extend(quantize_values(c, gots[c]) for c in range(2, BLOCKS))
+        def turn_values(n, v_bf, bank):
+            pairs = gots[n][:].bitcast(F32)
+            v_turned = psum.tile([P, 2, P], F32, name=f"v_turned{n}", tag=bank)
+            for u in range(2):
+                nc.tensor.transpose(v_turned[:, u, :], pairs[:, u : I // 2 : 2], ident[:])
+            nc.scalar.copy(
+                v_bf.bitcast(F32).rearrange("p (e u) -> p e u", u=2), v_turned[:].rearrange("p u e -> p e u")
+            )
+
+        operands = []
+        for pair, (bf_held_by, codes_held_by) in enumerate((("neg_max1", "vals3"), (None, "gain"))):
+            v_bf = sbuf([P, 2 * I], BF16, f"v_bf{pair}", tag=bf_held_by)
+            for side in range(2):
+                n = LOAD_ORDER.index(2 * pair + side)
+                turn_values(n, v_bf[:, side * I : (side + 1) * I], ("score0", "v_turned", "score1", "v_turned")[n])
+            v_codes = sbuf([P, 2 * P], U32, f"v_codes{pair}", tag=codes_held_by)
+            v_scales = sbuf([P, 2 * P], U8, f"v_scales{pair}")
+            nc.vector.quantize_mx(v_codes[:].bitcast(FP8X4), v_scales[:], v_bf[:])
+            operands.append((v_codes, v_scales))
 
         out_rows = out.rearrange("(h p) e -> p h e", p=P)
-        for c in range(BLOCKS):
-            v_codes, v_scales = quantized[c]
-            acc = psum.tile([P, HALVES, P], F32, name=f"acc{c}", tag=f"score{c % 2}")
-            for h in range(HALVES):
-                nc.tensor.matmul_mx(
-                    acc[:, h, :], lhsT=w_codes[:, h * P : (h + 1) * P].bitcast(FP8X4),
-                    lhsT_scale=w_scales[:, h * P : (h + 1) * P],
-                    rhs=v_codes[:].bitcast(FP8X4), rhs_scale=v_scales[:], start=True, stop=True,
-                )
-            result = sbuf([P, HALVES, P], F32, f"result{c}")
-            nc.scalar.copy(result[:], acc[:])
-            nc.sync.dma_start(out_rows[:, :, c * P : (c + 1) * P], result[:])
+
+        def multiply(acc, h, operand):
+            v_codes, v_scales = operand
+            nc.tensor.matmul_mx(
+                acc, lhsT=w_codes[:, h * P : (h + 1) * P].bitcast(FP8X4),
+                lhsT_scale=w_scales[:, h * P : (h + 1) * P],
+                rhs=v_codes[:].bitcast(FP8X4), rhs_scale=v_scales[:], start=True, stop=True,
+            )
+
+        width = E // 2
+        acc = psum.tile([P, HALVES, width], F32, name="acc_first", tag="acc_first")
+        for h in range(HALVES):
+            multiply(acc[:, h, :], h, operands[0])
+        result = sbuf([P, HALVES, width], F32, "result_first", tag="vals2")
+        nc.scalar.copy(result[:], acc[:])
+        nc.sync.dma_start(out_rows[:, :, :width], result[:])
+
+        for h in range(HALVES):
+            acc = psum.tile([P, width], F32, name=f"acc_last{h}", tag=f"score{h}")
+            multiply(acc[:], h, operands[1])
+            result = sbuf([P, width], F32, f"result_last{h}")
+            if h == 0:
+                nc.vector.tensor_copy(result[:], acc[:])
+                nc.sync.dma_start(out_rows[:, h, width:], result[:])
+            else:
+                nc.scalar.copy(result[:], acc[:])
+                nc.scalar.dma_start(out_rows[:, h, width:], result[:])

@@ -21,7 +21,8 @@ P = 128
 PACK = 4
 HALVES = Q // P
 BLOCKS = E // P
-LOAD_ORDER = (0, 2, 1, 3)
+PIECES = 4
+CUT = 384
 
 
 def tile_attend_sinkhorn_kernel(tc, query, keys_words, keys_scales, fac, vals, offs, out):
@@ -36,6 +37,15 @@ def tile_attend_sinkhorn_kernel(tc, query, keys_words, keys_scales, fac, vals, o
         offsets = keep.tile([P, I // 16], U16, name="offsets")
         nc.sync.dma_start(offsets[:], offs)
 
+        key_words = sbuf([P, T], U32, "key_words")
+        words_rows = keys_words[0].rearrange("p n t -> p (n t)").bitcast(I32)
+        nc.sync.dma_start(key_words[:, : T // 2].bitcast(I32), words_rows[:, : T // 2])
+
+        key_scales = sbuf([P, T], U8, "key_scales")
+        nc.gpsimd.memset(key_scales[:].bitcast(I32), 0)
+        for r in range(4):
+            nc.sync.dma_start(key_scales[r:P:32, :].bitcast(I32), keys_scales[0, r:16:4, :].bitcast(I32))
+
         query_rows = query.rearrange("(p j) q -> p j q", j=PACK)
 
         def load_query(h):
@@ -44,22 +54,32 @@ def tile_attend_sinkhorn_kernel(tc, query, keys_words, keys_scales, fac, vals, o
             return raw
 
         query_raw = [load_query(0)]
-
-        key_scales = sbuf([P, T], U8, "key_scales")
-        nc.vector.memset(key_scales[:].bitcast(I32), 0)
-        for quad in range(4):
-            nc.sync.dma_start(
-                key_scales[32 * quad : 32 * quad + 4, :].bitcast(I32),
-                keys_scales[0, 4 * quad : 4 * quad + 4, :].bitcast(I32),
-            )
-
-        key_words = sbuf([P, T], U32, "key_words")
-        nc.sync.dma_start(key_words[:].bitcast(I32), keys_words[0].rearrange("p n t -> p (n t)").bitcast(I32))
+        nc.sync.dma_start(key_words[:, T // 2 :].bitcast(I32), words_rows[:, T // 2 :])
         query_raw.append(load_query(1))
+
+        def load_values(block):
+            pool = sbuf([P, T], F32, f"vals{block}")
+            nc.sync.dma_start(pool[:], vals[block * P : (block + 1) * P, :])
+            return pool
+
+        span = T // PIECES
+
+        def load_piece(n):
+            piece = sbuf([P, span], F32, f"piece{n}")
+            nc.sync.dma_start(piece[:], vals[2 * P : 3 * P, n * span : (n + 1) * span])
+            return piece
+
+        pools = {0: load_values(0)}
+        fac_sb = sbuf([P, PACK], F32, "fac_sb")
+        nc.sync.dma_start(fac_sb[:], fac.rearrange("(p t) o -> p (t o)", t=PACK))
+        pieces = [load_piece(0), load_piece(1)]
+        pools[1] = load_values(1)
+        pieces.extend([load_piece(2), load_piece(3)])
+        pools[3] = load_values(3)
 
         warm = sbuf([P, 1], F32, "warm")
         warm_out = sbuf([P, 1], F32, "warm_out")
-        nc.gpsimd.memset(warm[:], 0.0)
+        nc.vector.memset(warm[:], 0.0)
         nc.scalar.activation(warm_out[:], warm[:], ACT.Exp)
 
         ident = sbuf([P, P], F32, "ident")
@@ -67,8 +87,9 @@ def tile_attend_sinkhorn_kernel(tc, query, keys_words, keys_scales, fac, vals, o
 
         got_scales = sbuf([P, I], U8, "got_scales")
         nc.vector.tensor_copy(got_scales[:], key_scales[:].indirect(offsets[:]))
-        got_words = sbuf([P, I], U32, "got_words")
-        nc.vector.tensor_copy(got_words[:], key_words[:].indirect(offsets[:]))
+        got_words = [sbuf([P, I // 2], U32, f"got_words{n}") for n in range(2)]
+        for n in range(2):
+            nc.vector.tensor_copy(got_words[n][:], key_words[:].indirect(offsets[:, 16 * n : 16 * (n + 1)]))
 
         scores = []
         for h in range(HALVES):
@@ -81,75 +102,66 @@ def tile_attend_sinkhorn_kernel(tc, query, keys_words, keys_scales, fac, vals, o
             q_scales = sbuf([P, P], U8, f"q_scales{h}")
             nc.vector.quantize_mx(q_codes[:].bitcast(FP8X4), q_scales[:], query_bf[:].rearrange("p q j -> p (q j)"))
             score = psum.tile([P, I], F32, name=f"score{h}", tag=f"score{h}")
-            nc.tensor.matmul_mx(
-                score[:], lhsT=q_codes[:].bitcast(FP8X4), lhsT_scale=q_scales[:],
-                rhs=got_words[:].bitcast(FP8X4), rhs_scale=got_scales[:], start=True, stop=True,
-            )
+            for n in range(2):
+                slots = slice(n * I // 2, (n + 1) * I // 2)
+                nc.tensor.matmul_mx(
+                    score[:, slots], lhsT=q_codes[:].bitcast(FP8X4), lhsT_scale=q_scales[:],
+                    rhs=got_words[n][:].bitcast(FP8X4), rhs_scale=got_scales[:, slots], start=True, stop=True,
+                )
             scores.append(score)
 
-        pools = []
-        for n, block in enumerate(LOAD_ORDER):
-            pool = sbuf([P, T], F32, f"vals{n}")
-            nc.sync.dma_start(pool[:], vals[block * P : (block + 1) * P, :])
-            pools.append(pool)
-            if n == 1:
-                fac_sb = sbuf([P, PACK], F32, "fac_sb")
-                nc.sync.dma_start(fac_sb[:], fac.rearrange("(p t) o -> p (t o)", t=PACK))
-
+        got0 = sbuf([P, I // 2], F32, "got_vals0")
+        got1 = sbuf([P, I // 2], F32, "got_vals1")
         expds, row_sums = [], []
         for h in range(HALVES):
-            neg_max = sbuf([P, 1], F32, f"neg_max{h}")
+            neg_max = sbuf([P, 1], F32, f"neg_max{h}", tag=("query_bf1", "neg_max1")[h])
             nc.vector.tensor_reduce(neg_max[:], scores[h][:], AXIS_X, ALU.max, negate=True)
             expd = sbuf([P, PACK, P], F32, f"expd{h}")
-            row_sum = sbuf([P, 1], F32, f"row_sum{h}")
+            row_sum = got0[:, 8 * h : 8 * h + 1]
             nc.scalar.activation(
                 expd[:], scores[h][:].rearrange("p (s t) -> p t s", t=PACK), ACT.Exp,
-                bias=neg_max[:], accum_out=row_sum[:],
+                bias=neg_max[:], accum_out=row_sum,
             )
             expds.append(expd)
             row_sums.append(row_sum)
         rows = []
         for h in range(HALVES):
-            row_inv = sbuf([P, 1], F32, f"row_inv{h}")
-            nc.vector.reciprocal(row_inv[:], row_sums[h][:])
+            row_inv = got1[:, 8 * h : 8 * h + 1]
+            nc.vector.reciprocal(row_inv, row_sums[h])
             row = sbuf([P, PACK, P], F32, f"row{h}")
-            nc.vector.tensor_scalar(row[:], expds[h][:], row_inv[:], None, ALU.mult)
+            nc.vector.tensor_scalar(row[:], expds[h][:], row_inv, None, ALU.mult)
             rows.append(row)
 
-        both = [psum.tile([P, 2, P], F32, name=f"both{u}", tag=f"turned{u}") for u in range(2)]
-        for h in range(HALVES):
-            for t in range(PACK):
-                nc.tensor.matmul(
-                    both[t // 2][:, t % 2, :], lhsT=rows[h][:, t, :], rhs=ident[:], is_transpose=True,
-                    start=(h == 0 and t % 2 == 0), stop=(h == HALVES - 1 and t % 2 == 1),
-                )
-
-        def gather_values(n, held_by):
-            got = sbuf([P, I], BF16, f"got_vals{n}", tag=held_by)
-            nc.vector.tensor_copy(got[:], pools[n][:].indirect(offsets[:]))
-            return got
-
-        gots = {0: gather_values(0, "expd1"), 2: gather_values(2, "vals0"), 3: gather_values(3, "vals2")}
-
-        vals_bf = sbuf([P, T], BF16, "vals_bf", tag="neg_max1")
-        nc.scalar.activation(vals_bf[:], pools[1][:], ACT.Copy)
-        gots[1] = sbuf([P, I], BF16, "got_vals1")
-        nc.scalar.activation(gots[1][:], vals_bf[:].indirect(offsets[:]), ACT.Copy)
-
-        col_sum = sbuf([P, PACK], F32, "col_sum")
-        summed = sbuf([P, P], BF16, "summed", tag="neg_max1")
-        for t in range(PACK):
-            nc.scalar.activation(summed[:], both[t // 2][:, t % 2, :], ACT.Copy, accum_out=col_sum[:, t : t + 1])
-
         turned = [psum.tile([P, PACK, P], F32, name=f"turned{h}", tag=f"turned{h}") for h in range(HALVES)]
-        for h in range(HALVES):
-            for t in range(PACK):
-                nc.tensor.transpose(turned[h][:, t, :], rows[h][:, t, :], ident[:])
+        for t in range(PACK):
+            nc.tensor.transpose(turned[0][:, t, :], rows[0][:, t, :], ident[:])
+        pair = [psum.tile([P, 2, P], F32, name=f"pair{u}", tag=("bank6", "bank7")[u]) for u in range(2)]
+        for t in range(PACK):
+            nc.tensor.transpose(pair[t // 2][:, t % 2, :], rows[1][:, t, :], ident[:])
+        for t in range(PACK):
+            nc.tensor.transpose(turned[1][:, t, :], rows[1][:, t, :], ident[:])
 
-        col_inv = sbuf([P, PACK], F32, "col_inv", tag="vals3")
-        nc.vector.reciprocal(col_inv[:], col_sum[:])
+        summed = sbuf([P, HALVES, PACK, P], BF16, "summed")
+        col_part = sbuf([P, PACK], F32, "col_part")
+        col_sum = got0[:, CUT // 2 : CUT // 2 + PACK]
+        for t in range(PACK):
+            nc.scalar.activation(
+                summed[:, 0, t, :], turned[0][:, t, :], ACT.Identity, scale=1.0 / P, accum_out=col_part[:, t : t + 1]
+            )
+        for t in range(PACK):
+            nc.scalar.activation(
+                summed[:, 1, t, :], pair[t // 2][:, t % 2, :], ACT.Identity, bias=col_part[:, t : t + 1],
+                accum_out=col_sum[:, t : t + 1],
+            )
+
+        nc.vector.tensor_copy(got0[:].bitcast(BF16)[:, :CUT], pools[0][:].indirect(offsets[:, : CUT // 16]))
+        nc.vector.tensor_copy(got1[:].bitcast(BF16), pools[1][:].indirect(offsets[:]))
+
+        col_inv = sbuf([P, PACK], F32, "col_inv", tag="vals1")
+        nc.vector.reciprocal(col_inv[:], col_sum)
         gain = sbuf([P, PACK], F32, "gain")
         nc.vector.tensor_tensor(gain[:], col_inv[:], fac_sb[:], ALU.mult)
+        nc.vector.tensor_copy(got0[:].bitcast(BF16)[:, CUT:], pools[0][:].indirect(offsets[:, CUT // 16 :]))
 
         w_bf = sbuf([P, HALVES, P, PACK], BF16, "w_bf")
         for h in range(HALVES):
@@ -157,29 +169,38 @@ def tile_attend_sinkhorn_kernel(tc, query, keys_words, keys_scales, fac, vals, o
                 w_bf[:, h], turned[h][:].rearrange("p t q -> p q t"),
                 gain[:].unsqueeze(1).to_broadcast([P, P, PACK]), ALU.mult,
             )
-        w_codes = sbuf([P, Q], U32, "w_codes")
-        w_scales = sbuf([P, Q], U8, "w_scales")
-        nc.vector.quantize_mx(w_codes[:].bitcast(FP8X4), w_scales[:], w_bf[:].rearrange("p h q t -> p (h q t)"))
-
-        def turn_values(n, v_bf, bank):
-            pairs = gots[n][:].bitcast(F32)
-            v_turned = psum.tile([P, 2, P], F32, name=f"v_turned{n}", tag=bank)
+        def turn_values(pairs, v_bf, bank):
+            v_turned = psum.tile([P, 2, P], F32, name="v_turned", tag=bank)
             for u in range(2):
                 nc.tensor.transpose(v_turned[:, u, :], pairs[:, u : I // 2 : 2], ident[:])
             nc.scalar.copy(
                 v_bf.bitcast(F32).rearrange("p (e u) -> p e u", u=2), v_turned[:].rearrange("p u e -> p e u")
             )
 
-        operands = []
-        for pair, (bf_held_by, codes_held_by) in enumerate((("neg_max1", "vals3"), (None, "gain"))):
-            v_bf = sbuf([P, 2 * I], BF16, f"v_bf{pair}", tag=bf_held_by)
-            for side in range(2):
-                n = LOAD_ORDER.index(2 * pair + side)
-                turn_values(n, v_bf[:, side * I : (side + 1) * I], ("score0", "v_turned", "score1", "v_turned")[n])
-            v_codes = sbuf([P, 2 * P], U32, f"v_codes{pair}", tag=codes_held_by)
-            v_scales = sbuf([P, 2 * P], U8, f"v_scales{pair}")
-            nc.vector.quantize_mx(v_codes[:].bitcast(FP8X4), v_scales[:], v_bf[:])
-            operands.append((v_codes, v_scales))
+        vals_bf = sbuf([P, T], BF16, "vals_bf", tag="neg_max1")
+        for n in range(PIECES):
+            nc.scalar.activation(vals_bf[:, n * span : (n + 1) * span], pieces[n][:], ACT.Copy)
+        got2 = sbuf([P, I // 2], F32, "got_vals2")
+        nc.scalar.activation(got2[:].bitcast(BF16), vals_bf[:].indirect(offsets[:]), ACT.Copy)
+
+        got3 = sbuf([P, I // 2], F32, "got_vals3")
+        nc.vector.tensor_copy(got3[:].bitcast(BF16), pools[3][:].indirect(offsets[:]))
+
+        v_bf = sbuf([P, BLOCKS * I], BF16, "v_bf", tag="neg_max1")
+        turn_values(got1[:], v_bf[:, I : 2 * I], "score0")
+        turn_values(got0[:], v_bf[:, :I], "bank5")
+        turn_values(got2[:], v_bf[:, 2 * I : 3 * I], "bank6")
+        turn_values(got3[:], v_bf[:, 3 * I :], "score1")
+
+        codes = sbuf([P, Q + E], U32, "codes", tag="vals3")
+        scales = sbuf([P, Q + E], U8, "scales")
+        w_codes, w_scales = codes[:, :Q], scales[:, :Q]
+        nc.vector.quantize_mx(w_codes.bitcast(FP8X4), w_scales, w_bf[:].rearrange("p h q t -> p (h q t)"))
+
+        def quantize_values(lo, hi):
+            v_codes, v_scales = codes[:, Q + lo : Q + hi], scales[:, Q + lo : Q + hi]
+            nc.vector.quantize_mx(v_codes.bitcast(FP8X4), v_scales, v_bf[:, PACK * lo : PACK * hi])
+            return v_codes, v_scales
 
         out_rows = out.rearrange("(h p) e -> p h e", p=P)
 
@@ -188,24 +209,24 @@ def tile_attend_sinkhorn_kernel(tc, query, keys_words, keys_scales, fac, vals, o
             nc.tensor.matmul_mx(
                 acc, lhsT=w_codes[:, h * P : (h + 1) * P].bitcast(FP8X4),
                 lhsT_scale=w_scales[:, h * P : (h + 1) * P],
-                rhs=v_codes[:].bitcast(FP8X4), rhs_scale=v_scales[:], start=True, stop=True,
+                rhs=v_codes.bitcast(FP8X4), rhs_scale=v_scales, start=True, stop=True,
             )
 
-        width = E // 2
-        acc = psum.tile([P, HALVES, width], F32, name="acc_first", tag="acc_first")
-        for h in range(HALVES):
-            multiply(acc[:, h, :], h, operands[0])
-        result = sbuf([P, HALVES, width], F32, "result_first", tag="vals2")
-        nc.scalar.copy(result[:], acc[:])
-        nc.sync.dma_start(out_rows[:, :, :width], result[:])
+        first = quantize_values(0, 2 * P)
+        third = quantize_values(2 * P, 3 * P)
+        last = quantize_values(3 * P, E)
 
         for h in range(HALVES):
-            acc = psum.tile([P, width], F32, name=f"acc_last{h}", tag=f"score{h}")
-            multiply(acc[:], h, operands[1])
-            result = sbuf([P, width], F32, f"result_last{h}")
-            if h == 0:
-                nc.vector.tensor_copy(result[:], acc[:])
-                nc.sync.dma_start(out_rows[:, h, width:], result[:])
-            else:
-                nc.scalar.copy(result[:], acc[:])
-                nc.scalar.dma_start(out_rows[:, h, width:], result[:])
+            acc = psum.tile([P, 2 * P], F32, name="acc_first", tag=("bank7", "turned1")[h])
+            multiply(acc[:], h, first)
+            result = sbuf([P, 2 * P], F32, f"result_first{h}")
+            nc.scalar.copy(result[:], acc[:])
+            nc.sync.dma_start(out_rows[:, h, : 2 * P], result[:])
+
+        for block, operand, bank in ((2, third, "bank5"), (3, last, "turned0")):
+            acc = psum.tile([P, HALVES, P], F32, name="acc", tag=bank)
+            for h in range(HALVES):
+                multiply(acc[:, h, :], h, operand)
+            result = sbuf([P, HALVES, P], F32, f"result{block}")
+            nc.vector.tensor_copy(result[:], acc[:])
+            nc.sync.dma_start(out_rows[:, :, block * P : (block + 1) * P], result[:])

@@ -21,7 +21,7 @@ P = 128
 PACK = 4
 HALVES = Q // P
 BLOCKS = E // P
-PIECES = 4
+PIECES = 2
 CUT = 384
 
 
@@ -71,10 +71,10 @@ def tile_attend_sinkhorn_kernel(tc, query, keys_words, keys_scales, fac, vals, o
 
         pools = {0: load_values(0)}
         fac_sb = sbuf([P, PACK], F32, "fac_sb")
-        nc.sync.dma_start(fac_sb[:], fac.rearrange("(p t) o -> p (t o)", t=PACK))
-        pieces = [load_piece(0), load_piece(1)]
+        nc.gpsimd.dma_start(fac_sb[:], fac.rearrange("(p t) o -> p (t o)", t=PACK))
+        pieces = [load_piece(0)]
         pools[1] = load_values(1)
-        pieces.extend([load_piece(2), load_piece(3)])
+        pieces.append(load_piece(1))
         pools[3] = load_values(3)
 
         warm = sbuf([P, 1], F32, "warm")
@@ -166,8 +166,9 @@ def tile_attend_sinkhorn_kernel(tc, query, keys_words, keys_scales, fac, vals, o
         w_bf = sbuf([P, HALVES, P, PACK], BF16, "w_bf")
         for h in range(HALVES):
             nc.vector.tensor_tensor(
-                w_bf[:, h], turned[h][:].rearrange("p t q -> p q t"),
-                gain[:].unsqueeze(1).to_broadcast([P, P, PACK]), ALU.mult,
+                w_bf[:, h].rearrange("p (c i) t -> p c t i", i=4),
+                turned[h][:].rearrange("p t (c i) -> p c t i", i=4),
+                gain[:].unsqueeze(1).unsqueeze(3).to_broadcast([P, P // 4, PACK, 4]), ALU.mult,
             )
         def turn_values(pairs, v_bf, bank):
             v_turned = psum.tile([P, 2, P], F32, name="v_turned", tag=bank)

@@ -22,7 +22,8 @@ PACK = 4
 HALVES = Q // P
 BLOCKS = E // P
 PIECES = 2
-CUT = 384
+CUT = 128
+HUGE = 2.0**126
 
 
 def tile_attend_sinkhorn_kernel(tc, query, keys_words, keys_scales, fac, vals, offs, out):
@@ -34,12 +35,12 @@ def tile_attend_sinkhorn_kernel(tc, query, keys_words, keys_scales, fac, vals, o
         def sbuf(shape, dtype, name, tag=None):
             return keep.tile(shape, dtype, name=name, tag=tag or name, align_bytes=64)
 
-        offsets = keep.tile([P, I // 16], U16, name="offsets")
-        nc.sync.dma_start(offsets[:], offs)
-
         key_words = sbuf([P, T], U32, "key_words")
         words_rows = keys_words[0].rearrange("p n t -> p (n t)").bitcast(I32)
         nc.sync.dma_start(key_words[:, : T // 2].bitcast(I32), words_rows[:, : T // 2])
+
+        offsets = keep.tile([P, I // 16], U16, name="offsets")
+        nc.sync.dma_start(offsets[:], offs)
 
         key_scales = sbuf([P, T], U8, "key_scales")
         nc.gpsimd.memset(key_scales[:].bitcast(I32), 0)
@@ -112,18 +113,26 @@ def tile_attend_sinkhorn_kernel(tc, query, keys_words, keys_scales, fac, vals, o
 
         got0 = sbuf([P, I // 2], F32, "got_vals0")
         got1 = sbuf([P, I // 2], F32, "got_vals1")
+        small = sbuf([P, 16], F32, "small", tag="query_bf1")
         expds, row_sums = [], []
         for h in range(HALVES):
-            neg_max = sbuf([P, 1], F32, f"neg_max{h}", tag=("query_bf1", "neg_max1")[h])
-            nc.vector.tensor_reduce(neg_max[:], scores[h][:], AXIS_X, ALU.max, negate=True)
+            neg_max = small[:, 0:1] if h == 0 else sbuf([P, 1], F32, "neg_max1")[:]
+            nc.vector.tensor_reduce(neg_max, scores[h][:], AXIS_X, ALU.max, negate=True)
             expd = sbuf([P, PACK, P], F32, f"expd{h}")
-            row_sum = got0[:, 8 * h : 8 * h + 1]
+            row_sum = got0[:, P + 8 * h : P + 8 * h + 1]
             nc.scalar.activation(
                 expd[:], scores[h][:].rearrange("p (s t) -> p t s", t=PACK), ACT.Exp,
-                bias=neg_max[:], accum_out=row_sum,
+                bias=neg_max, accum_out=row_sum,
             )
             expds.append(expd)
             row_sums.append(row_sum)
+        fac_raw_inv = small[:, 8 : 8 + PACK]
+        nc.vector.reciprocal(fac_raw_inv, fac_sb[:])
+        fac_inv = sbuf([P, PACK], F32, "fac_inv")
+        nc.gpsimd.tensor_scalar(fac_inv[:], fac_raw_inv, HUGE, -HUGE, ALU.min, ALU.max)
+        fac_inv_mean = sbuf([P, PACK], F32, "fac_inv_mean")
+        nc.gpsimd.tensor_scalar(fac_inv_mean[:], fac_inv[:], 1.0 / P, 0.0, ALU.mult, ALU.add)
+
         rows = []
         for h in range(HALVES):
             row_inv = got1[:, 8 * h : 8 * h + 1]
@@ -143,32 +152,30 @@ def tile_attend_sinkhorn_kernel(tc, query, keys_words, keys_scales, fac, vals, o
 
         summed = sbuf([P, HALVES, PACK, P], BF16, "summed")
         col_part = sbuf([P, PACK], F32, "col_part")
-        col_sum = got0[:, CUT // 2 : CUT // 2 + PACK]
+        col_sum = sbuf([P, PACK], F32, "col_sum")
         for t in range(PACK):
             nc.scalar.activation(
-                summed[:, 0, t, :], turned[0][:, t, :], ACT.Identity, scale=1.0 / P, accum_out=col_part[:, t : t + 1]
+                summed[:, 0, t, :], turned[0][:, t, :], ACT.Identity, scale=fac_inv_mean[:, t : t + 1],
+                accum_out=col_part[:, t : t + 1],
             )
         for t in range(PACK):
             nc.scalar.activation(
                 summed[:, 1, t, :], pair[t // 2][:, t % 2, :], ACT.Identity, bias=col_part[:, t : t + 1],
-                accum_out=col_sum[:, t : t + 1],
+                scale=fac_inv[:, t : t + 1], accum_out=col_sum[:, t : t + 1],
             )
 
         nc.vector.tensor_copy(got0[:].bitcast(BF16)[:, :CUT], pools[0][:].indirect(offsets[:, : CUT // 16]))
+        nc.vector.tensor_copy(got0[:].bitcast(BF16)[:, CUT:], pools[0][:].indirect(offsets[:, CUT // 16 :]))
         nc.vector.tensor_copy(got1[:].bitcast(BF16), pools[1][:].indirect(offsets[:]))
 
-        col_inv = sbuf([P, PACK], F32, "col_inv", tag="vals1")
-        nc.vector.reciprocal(col_inv[:], col_sum)
-        gain = sbuf([P, PACK], F32, "gain")
-        nc.vector.tensor_tensor(gain[:], col_inv[:], fac_sb[:], ALU.mult)
-        nc.vector.tensor_copy(got0[:].bitcast(BF16)[:, CUT:], pools[0][:].indirect(offsets[:, CUT // 16 :]))
+        gain = sbuf([P, PACK], F32, "gain", tag="vals1")
+        nc.vector.reciprocal(gain[:], col_sum[:])
 
         w_bf = sbuf([P, HALVES, P, PACK], BF16, "w_bf")
         for h in range(HALVES):
             nc.vector.tensor_tensor(
-                w_bf[:, h].rearrange("p (c i) t -> p c t i", i=4),
-                turned[h][:].rearrange("p t (c i) -> p c t i", i=4),
-                gain[:].unsqueeze(1).unsqueeze(3).to_broadcast([P, P // 4, PACK, 4]), ALU.mult,
+                w_bf[:, h], turned[h][:].rearrange("p t q -> p q t"),
+                gain[:].unsqueeze(1).to_broadcast([P, P, PACK]), ALU.mult,
             )
         def turn_values(pairs, v_bf, bank):
             v_turned = psum.tile([P, 2, P], F32, name="v_turned", tag=bank)
@@ -193,13 +200,17 @@ def tile_attend_sinkhorn_kernel(tc, query, keys_words, keys_scales, fac, vals, o
         turn_values(got2[:], v_bf[:, 2 * I : 3 * I], "bank6")
         turn_values(got3[:], v_bf[:, 3 * I :], "score1")
 
-        codes = sbuf([P, Q + E], U32, "codes", tag="vals3")
-        scales = sbuf([P, Q + E], U8, "scales")
-        w_codes, w_scales = codes[:, :Q], scales[:, :Q]
-        nc.vector.quantize_mx(w_codes.bitcast(FP8X4), w_scales, w_bf[:].rearrange("p h q t -> p (h q t)"))
+        codes = sbuf([P, P + E], U32, "codes", tag="vals3")
+        scales = sbuf([P, P + E], U8, "scales")
+        early_codes = sbuf([P, P], U32, "early_codes")
+        early_scales = sbuf([P, P], U8, "early_scales")
+        w_codes, w_scales = (early_codes[:], codes[:, E:]), (early_scales[:], scales[:, E:])
+
+        def quantize_weights(h):
+            nc.vector.quantize_mx(w_codes[h].bitcast(FP8X4), w_scales[h], w_bf[:, h].rearrange("p q t -> p (q t)"))
 
         def quantize_values(lo, hi):
-            v_codes, v_scales = codes[:, Q + lo : Q + hi], scales[:, Q + lo : Q + hi]
+            v_codes, v_scales = codes[:, lo:hi], scales[:, lo:hi]
             nc.vector.quantize_mx(v_codes.bitcast(FP8X4), v_scales, v_bf[:, PACK * lo : PACK * hi])
             return v_codes, v_scales
 
@@ -208,12 +219,13 @@ def tile_attend_sinkhorn_kernel(tc, query, keys_words, keys_scales, fac, vals, o
         def multiply(acc, h, operand):
             v_codes, v_scales = operand
             nc.tensor.matmul_mx(
-                acc, lhsT=w_codes[:, h * P : (h + 1) * P].bitcast(FP8X4),
-                lhsT_scale=w_scales[:, h * P : (h + 1) * P],
+                acc, lhsT=w_codes[h].bitcast(FP8X4), lhsT_scale=w_scales[h],
                 rhs=v_codes.bitcast(FP8X4), rhs_scale=v_scales, start=True, stop=True,
             )
 
+        quantize_weights(0)
         first = quantize_values(0, 2 * P)
+        quantize_weights(1)
         third = quantize_values(2 * P, 3 * P)
         last = quantize_values(3 * P, E)
 
@@ -224,10 +236,20 @@ def tile_attend_sinkhorn_kernel(tc, query, keys_words, keys_scales, fac, vals, o
             nc.scalar.copy(result[:], acc[:])
             nc.sync.dma_start(out_rows[:, h, : 2 * P], result[:])
 
-        for block, operand, bank in ((2, third, "bank5"), (3, last, "turned0")):
-            acc = psum.tile([P, HALVES, P], F32, name="acc", tag=bank)
-            for h in range(HALVES):
-                multiply(acc[:, h, :], h, operand)
-            result = sbuf([P, HALVES, P], F32, f"result{block}")
-            nc.vector.tensor_copy(result[:], acc[:])
-            nc.sync.dma_start(out_rows[:, :, block * P : (block + 1) * P], result[:])
+        acc = psum.tile([P, HALVES, P], F32, name="acc_third", tag="bank5")
+        for h in range(HALVES):
+            multiply(acc[:, h, :], h, third)
+        result = sbuf([P, HALVES, P], F32, "result_third")
+        nc.vector.tensor_copy(result[:], acc[:])
+        nc.sync.dma_start(out_rows[:, :, 2 * P : 3 * P], result[:])
+
+        for h in range(HALVES):
+            acc = psum.tile([P, P], F32, name="acc_last", tag=("turned0", "score0")[h])
+            multiply(acc[:], h, last)
+            result = sbuf([P, P], F32, f"result_last{h}")
+            if h == 0:
+                nc.scalar.copy(result[:], acc[:])
+                nc.scalar.dma_start(out_rows[:, h, 3 * P :], result[:])
+            else:
+                nc.vector.tensor_copy(result[:], acc[:])
+                nc.sync.dma_start(out_rows[:, h, 3 * P :], result[:])

@@ -21,8 +21,8 @@ P = 128
 PACK = 4
 HALVES = Q // P
 BLOCKS = E // P
-PIECES = 2
-CUT = 128
+PIECES = 4
+CUTS = (0, 128, 512)
 HUGE = 2.0**126
 
 
@@ -70,12 +70,12 @@ def tile_attend_sinkhorn_kernel(tc, query, keys_words, keys_scales, fac, vals, o
             nc.sync.dma_start(piece[:], vals[2 * P : 3 * P, n * span : (n + 1) * span])
             return piece
 
-        pools = {0: load_values(0)}
         fac_sb = sbuf([P, PACK], F32, "fac_sb")
-        nc.gpsimd.dma_start(fac_sb[:], fac.rearrange("(p t) o -> p (t o)", t=PACK))
-        pieces = [load_piece(0)]
+        nc.sync.dma_start(fac_sb[:], fac.rearrange("(p t) o -> p (t o)", t=PACK))
+        pools = {0: load_values(0)}
+        pieces = [load_piece(0), load_piece(1)]
         pools[1] = load_values(1)
-        pieces.append(load_piece(1))
+        pieces.extend(load_piece(n) for n in range(2, PIECES))
         pools[3] = load_values(3)
 
         warm = sbuf([P, 1], F32, "warm")
@@ -130,8 +130,6 @@ def tile_attend_sinkhorn_kernel(tc, query, keys_words, keys_scales, fac, vals, o
         nc.vector.reciprocal(fac_raw_inv, fac_sb[:])
         fac_inv = sbuf([P, PACK], F32, "fac_inv")
         nc.gpsimd.tensor_scalar(fac_inv[:], fac_raw_inv, HUGE, -HUGE, ALU.min, ALU.max)
-        fac_inv_mean = sbuf([P, PACK], F32, "fac_inv_mean")
-        nc.gpsimd.tensor_scalar(fac_inv_mean[:], fac_inv[:], 1.0 / P, 0.0, ALU.mult, ALU.add)
 
         rows = []
         for h in range(HALVES):
@@ -141,38 +139,34 @@ def tile_attend_sinkhorn_kernel(tc, query, keys_words, keys_scales, fac, vals, o
             nc.vector.tensor_scalar(row[:], expds[h][:], row_inv, None, ALU.mult)
             rows.append(row)
 
-        turned = [psum.tile([P, PACK, P], F32, name=f"turned{h}", tag=f"turned{h}") for h in range(HALVES)]
-        for t in range(PACK):
-            nc.tensor.transpose(turned[0][:, t, :], rows[0][:, t, :], ident[:])
-        pair = [psum.tile([P, 2, P], F32, name=f"pair{u}", tag=("bank6", "bank7")[u]) for u in range(2)]
-        for t in range(PACK):
-            nc.tensor.transpose(pair[t // 2][:, t % 2, :], rows[1][:, t, :], ident[:])
-        for t in range(PACK):
-            nc.tensor.transpose(turned[1][:, t, :], rows[1][:, t, :], ident[:])
+        both = [psum.tile([P, P], F32, name=f"both{t}", tag=("bank6", "bank7", "bank8", "score0")[t]) for t in range(PACK)]
+        for h in range(HALVES):
+            for t in range(PACK):
+                nc.tensor.matmul(
+                    both[t][:], lhsT=rows[h][:, t, :], rhs=ident[:], is_transpose=True, start=(h == 0), stop=(h == 1)
+                )
 
-        summed = sbuf([P, HALVES, PACK, P], BF16, "summed")
-        col_part = sbuf([P, PACK], F32, "col_part")
+        summed = sbuf([P, PACK, P], BF16, "summed")
         col_sum = sbuf([P, PACK], F32, "col_sum")
         for t in range(PACK):
             nc.scalar.activation(
-                summed[:, 0, t, :], turned[0][:, t, :], ACT.Identity, scale=fac_inv_mean[:, t : t + 1],
-                accum_out=col_part[:, t : t + 1],
-            )
-        for t in range(PACK):
-            nc.scalar.activation(
-                summed[:, 1, t, :], pair[t // 2][:, t % 2, :], ACT.Identity, bias=col_part[:, t : t + 1],
-                scale=fac_inv[:, t : t + 1], accum_out=col_sum[:, t : t + 1],
+                summed[:, t, :], both[t][:], ACT.Copy, scale=fac_inv[:, t : t + 1], accum_out=col_sum[:, t : t + 1]
             )
 
-        nc.vector.tensor_copy(got0[:].bitcast(BF16)[:, :CUT], pools[0][:].indirect(offsets[:, : CUT // 16]))
-        nc.vector.tensor_copy(got0[:].bitcast(BF16)[:, CUT:], pools[0][:].indirect(offsets[:, CUT // 16 :]))
+        turned = [psum.tile([P, PACK, P], F32, name=f"turned{h}", tag=("bank6", "turned1")[h]) for h in range(HALVES)]
+        for h in (1, 0):
+            for t in range(PACK):
+                nc.tensor.transpose(turned[h][:, t, :], rows[h][:, t, :], ident[:])
+
+        for lo, hi in zip(CUTS, CUTS[1:]):
+            nc.vector.tensor_copy(got0[:].bitcast(BF16)[:, lo:hi], pools[0][:].indirect(offsets[:, lo // 16 : hi // 16]))
         nc.vector.tensor_copy(got1[:].bitcast(BF16), pools[1][:].indirect(offsets[:]))
 
         gain = sbuf([P, PACK], F32, "gain", tag="vals1")
         nc.vector.reciprocal(gain[:], col_sum[:])
 
         w_bf = sbuf([P, HALVES, P, PACK], BF16, "w_bf")
-        for h in range(HALVES):
+        for h in (1, 0):
             nc.vector.tensor_tensor(
                 w_bf[:, h], turned[h][:].rearrange("p t q -> p q t"),
                 gain[:].unsqueeze(1).to_broadcast([P, P, PACK]), ALU.mult,
@@ -204,7 +198,7 @@ def tile_attend_sinkhorn_kernel(tc, query, keys_words, keys_scales, fac, vals, o
         scales = sbuf([P, P + E], U8, "scales")
         early_codes = sbuf([P, P], U32, "early_codes")
         early_scales = sbuf([P, P], U8, "early_scales")
-        w_codes, w_scales = (early_codes[:], codes[:, E:]), (early_scales[:], scales[:, E:])
+        w_codes, w_scales = (codes[:, E:], early_codes[:]), (scales[:, E:], early_scales[:])
 
         def quantize_weights(h):
             nc.vector.quantize_mx(w_codes[h].bitcast(FP8X4), w_scales[h], w_bf[:, h].rearrange("p q t -> p (q t)"))
@@ -223,33 +217,23 @@ def tile_attend_sinkhorn_kernel(tc, query, keys_words, keys_scales, fac, vals, o
                 rhs=v_codes.bitcast(FP8X4), rhs_scale=v_scales, start=True, stop=True,
             )
 
-        quantize_weights(0)
-        first = quantize_values(0, 2 * P)
         quantize_weights(1)
+        first = quantize_values(0, 2 * P)
+        quantize_weights(0)
         third = quantize_values(2 * P, 3 * P)
         last = quantize_values(3 * P, E)
 
-        for h in range(HALVES):
+        for h in (1, 0):
             acc = psum.tile([P, 2 * P], F32, name="acc_first", tag=("bank7", "turned1")[h])
             multiply(acc[:], h, first)
             result = sbuf([P, 2 * P], F32, f"result_first{h}")
             nc.scalar.copy(result[:], acc[:])
             nc.sync.dma_start(out_rows[:, h, : 2 * P], result[:])
 
-        acc = psum.tile([P, HALVES, P], F32, name="acc_third", tag="bank5")
-        for h in range(HALVES):
-            multiply(acc[:, h, :], h, third)
-        result = sbuf([P, HALVES, P], F32, "result_third")
-        nc.vector.tensor_copy(result[:], acc[:])
-        nc.sync.dma_start(out_rows[:, :, 2 * P : 3 * P], result[:])
-
-        for h in range(HALVES):
-            acc = psum.tile([P, P], F32, name="acc_last", tag=("turned0", "score0")[h])
-            multiply(acc[:], h, last)
-            result = sbuf([P, P], F32, f"result_last{h}")
-            if h == 0:
-                nc.scalar.copy(result[:], acc[:])
-                nc.scalar.dma_start(out_rows[:, h, 3 * P :], result[:])
-            else:
-                nc.vector.tensor_copy(result[:], acc[:])
-                nc.sync.dma_start(out_rows[:, h, 3 * P :], result[:])
+        for block, operand, bank in ((2, third, "bank5"), (3, last, "turned0")):
+            acc = psum.tile([P, HALVES, P], F32, name="acc", tag=bank)
+            for h in range(HALVES):
+                multiply(acc[:, h, :], h, operand)
+            result = sbuf([P, HALVES, P], F32, f"result{block}")
+            nc.vector.tensor_copy(result[:], acc[:])
+            nc.sync.dma_start(out_rows[:, :, block * P : (block + 1) * P], result[:])

@@ -19,11 +19,15 @@ AXIS_X = mybir.AxisListType.X
 
 P = 128
 PACK = 4
+LIST_ROWS = 16
 HALVES = Q // P
 BLOCKS = E // P
+PAIRS = I // 2
+APART = 8
 PIECES = 4
-CUTS = (0, 128, 512)
-HUGE = 2.0**126
+EARLY_SLOTS = 128
+LARGEST_FACTOR = 2.0**126
+HALF_ORDER = (1, 0)
 
 
 def tile_attend_sinkhorn_kernel(tc, query, keys_words, keys_scales, fac, vals, offs, out):
@@ -35,11 +39,14 @@ def tile_attend_sinkhorn_kernel(tc, query, keys_words, keys_scales, fac, vals, o
         def sbuf(shape, dtype, name, tag=None):
             return keep.tile(shape, dtype, name=name, tag=tag or name, align_bytes=64)
 
+        def bank(number, shape, name):
+            return psum.tile(shape, F32, name=name, tag=f"bank{number}")
+
         key_words = sbuf([P, T], U32, "key_words")
         words_rows = keys_words[0].rearrange("p n t -> p (n t)").bitcast(I32)
         nc.sync.dma_start(key_words[:, : T // 2].bitcast(I32), words_rows[:, : T // 2])
 
-        offsets = keep.tile([P, I // 16], U16, name="offsets")
+        offsets = keep.tile([P, I // LIST_ROWS], U16, name="offsets")
         nc.sync.dma_start(offsets[:], offs)
 
         key_scales = sbuf([P, T], U8, "key_scales")
@@ -73,25 +80,21 @@ def tile_attend_sinkhorn_kernel(tc, query, keys_words, keys_scales, fac, vals, o
         fac_sb = sbuf([P, PACK], F32, "fac_sb")
         nc.sync.dma_start(fac_sb[:], fac.rearrange("(p t) o -> p (t o)", t=PACK))
         pools = {0: load_values(0)}
-        pieces = [load_piece(0), load_piece(1)]
+        pieces = [load_piece(n) for n in range(PIECES // 2)]
         pools[1] = load_values(1)
-        pieces.extend(load_piece(n) for n in range(2, PIECES))
+        pieces.extend(load_piece(n) for n in range(PIECES // 2, PIECES))
         pools[3] = load_values(3)
-
-        warm = sbuf([P, 1], F32, "warm")
-        warm_out = sbuf([P, 1], F32, "warm_out")
-        nc.vector.memset(warm[:], 0.0)
-        nc.scalar.activation(warm_out[:], warm[:], ACT.Exp)
 
         ident = sbuf([P, P], F32, "ident")
         make_identity(nc, ident[:])
 
-        got_scales = sbuf([P, I], U8, "got_scales")
-        nc.vector.tensor_copy(got_scales[:], key_scales[:].indirect(offsets[:]))
-        got_words = [sbuf([P, I // 2], U32, f"got_words{n}") for n in range(2)]
-        for n in range(2):
-            nc.vector.tensor_copy(got_words[n][:], key_words[:].indirect(offsets[:, 16 * n : 16 * (n + 1)]))
+        def listed(window, first_slot, end_slot):
+            return window[:].indirect(offsets[:, first_slot // LIST_ROWS : end_slot // LIST_ROWS])
 
+        got_scales = sbuf([P, I], U8, "got_scales")
+        nc.vector.tensor_copy(got_scales[:], listed(key_scales, 0, I))
+
+        slot_runs = (slice(0, I // 2), slice(I // 2, I))
         scores = []
         for h in range(HALVES):
             query_bf = sbuf([P, P, PACK], BF16, f"query_bf{h}")
@@ -102,138 +105,143 @@ def tile_attend_sinkhorn_kernel(tc, query, keys_words, keys_scales, fac, vals, o
             q_codes = sbuf([P, P], U32, f"q_codes{h}")
             q_scales = sbuf([P, P], U8, f"q_scales{h}")
             nc.vector.quantize_mx(q_codes[:].bitcast(FP8X4), q_scales[:], query_bf[:].rearrange("p q j -> p (q j)"))
-            score = psum.tile([P, I], F32, name=f"score{h}", tag=f"score{h}")
-            for n in range(2):
-                slots = slice(n * I // 2, (n + 1) * I // 2)
+            if h == 0:
+                got_words = sbuf([P, I], U32, "got_words", tag="query_bf0")
+                for run in slot_runs:
+                    nc.vector.tensor_copy(got_words[:, run], listed(key_words, run.start, run.stop))
+            score = bank(h, [P, I], f"score{h}")
+            for run in slot_runs:
                 nc.tensor.matmul_mx(
-                    score[:, slots], lhsT=q_codes[:].bitcast(FP8X4), lhsT_scale=q_scales[:],
-                    rhs=got_words[n][:].bitcast(FP8X4), rhs_scale=got_scales[:, slots], start=True, stop=True,
+                    score[:, run], lhsT=q_codes[:].bitcast(FP8X4), lhsT_scale=q_scales[:],
+                    rhs=got_words[:, run].bitcast(FP8X4), rhs_scale=got_scales[:, run], start=True, stop=True,
                 )
             scores.append(score)
 
-        got0 = sbuf([P, I // 2], F32, "got_vals0")
-        got1 = sbuf([P, I // 2], F32, "got_vals1")
-        small = sbuf([P, 16], F32, "small", tag="query_bf1")
+        got0 = sbuf([P, PAIRS], F32, "got_vals0")
+        got1 = sbuf([P, PAIRS], F32, "got_vals1")
+        behind_query = sbuf([P, 2 * APART], F32, "behind_query", tag="query_bf1")
+
         expds, row_sums = [], []
         for h in range(HALVES):
-            neg_max = small[:, 0:1] if h == 0 else sbuf([P, 1], F32, "neg_max1")[:]
+            neg_max = behind_query[:, 0:1] if h == 0 else sbuf([P, 1], F32, "neg_max1")[:]
             nc.vector.tensor_reduce(neg_max, scores[h][:], AXIS_X, ALU.max, negate=True)
             expd = sbuf([P, PACK, P], F32, f"expd{h}")
-            row_sum = got0[:, P + 8 * h : P + 8 * h + 1]
+            column = PAIRS // 2 + APART * h
+            row_sum = got0[:, column : column + 1]
             nc.scalar.activation(
                 expd[:], scores[h][:].rearrange("p (s t) -> p t s", t=PACK), ACT.Exp,
                 bias=neg_max, accum_out=row_sum,
             )
             expds.append(expd)
             row_sums.append(row_sum)
-        fac_raw_inv = small[:, 8 : 8 + PACK]
-        nc.vector.reciprocal(fac_raw_inv, fac_sb[:])
+        fac_inv_raw = behind_query[:, APART : APART + PACK]
+        nc.vector.reciprocal(fac_inv_raw, fac_sb[:])
         fac_inv = sbuf([P, PACK], F32, "fac_inv")
-        nc.gpsimd.tensor_scalar(fac_inv[:], fac_raw_inv, HUGE, -HUGE, ALU.min, ALU.max)
+        nc.gpsimd.tensor_scalar(fac_inv[:], fac_inv_raw, LARGEST_FACTOR, -LARGEST_FACTOR, ALU.min, ALU.max)
 
         rows = []
         for h in range(HALVES):
-            row_inv = got1[:, 8 * h : 8 * h + 1]
+            row_inv = got1[:, APART * h : APART * h + 1]
             nc.vector.reciprocal(row_inv, row_sums[h])
             row = sbuf([P, PACK, P], F32, f"row{h}")
             nc.vector.tensor_scalar(row[:], expds[h][:], row_inv, None, ALU.mult)
             rows.append(row)
 
-        both = [psum.tile([P, P], F32, name=f"both{t}", tag=("bank6", "bank7", "bank8", "score0")[t]) for t in range(PACK)]
+        both = [bank((2, 3, 4, 0)[t], [P, P], f"both{t}") for t in range(PACK)]
         for h in range(HALVES):
             for t in range(PACK):
                 nc.tensor.matmul(
-                    both[t][:], lhsT=rows[h][:, t, :], rhs=ident[:], is_transpose=True, start=(h == 0), stop=(h == 1)
+                    both[t][:], lhsT=rows[h][:, t, :], rhs=ident[:], is_transpose=True,
+                    start=(h == 0), stop=(h == HALVES - 1),
                 )
 
-        summed = sbuf([P, PACK, P], BF16, "summed")
+        scaled = sbuf([P, PACK, P], BF16, "scaled")
         col_sum = sbuf([P, PACK], F32, "col_sum")
         for t in range(PACK):
             nc.scalar.activation(
-                summed[:, t, :], both[t][:], ACT.Copy, scale=fac_inv[:, t : t + 1], accum_out=col_sum[:, t : t + 1]
+                scaled[:, t, :], both[t][:], ACT.Copy, scale=fac_inv[:, t : t + 1], accum_out=col_sum[:, t : t + 1]
             )
 
-        turned = [psum.tile([P, PACK, P], F32, name=f"turned{h}", tag=("bank6", "turned1")[h]) for h in range(HALVES)]
-        for h in (1, 0):
+        turned = [bank((2, 5)[h], [P, PACK, P], f"turned{h}") for h in range(HALVES)]
+        for h in HALF_ORDER:
             for t in range(PACK):
                 nc.tensor.transpose(turned[h][:, t, :], rows[h][:, t, :], ident[:])
 
-        for lo, hi in zip(CUTS, CUTS[1:]):
-            nc.vector.tensor_copy(got0[:].bitcast(BF16)[:, lo:hi], pools[0][:].indirect(offsets[:, lo // 16 : hi // 16]))
-        nc.vector.tensor_copy(got1[:].bitcast(BF16), pools[1][:].indirect(offsets[:]))
+        for first_slot, end_slot in ((0, EARLY_SLOTS), (EARLY_SLOTS, I)):
+            nc.vector.tensor_copy(got0[:].bitcast(BF16)[:, first_slot:end_slot], listed(pools[0], first_slot, end_slot))
+        nc.vector.tensor_copy(got1[:].bitcast(BF16), listed(pools[1], 0, I))
 
         gain = sbuf([P, PACK], F32, "gain", tag="vals1")
         nc.vector.reciprocal(gain[:], col_sum[:])
 
         w_bf = sbuf([P, HALVES, P, PACK], BF16, "w_bf")
-        for h in (1, 0):
+        for h in HALF_ORDER:
             nc.vector.tensor_tensor(
                 w_bf[:, h], turned[h][:].rearrange("p t q -> p q t"),
                 gain[:].unsqueeze(1).to_broadcast([P, P, PACK]), ALU.mult,
-            )
-        def turn_values(pairs, v_bf, bank):
-            v_turned = psum.tile([P, 2, P], F32, name="v_turned", tag=bank)
-            for u in range(2):
-                nc.tensor.transpose(v_turned[:, u, :], pairs[:, u : I // 2 : 2], ident[:])
-            nc.scalar.copy(
-                v_bf.bitcast(F32).rearrange("p (e u) -> p e u", u=2), v_turned[:].rearrange("p u e -> p e u")
             )
 
         vals_bf = sbuf([P, T], BF16, "vals_bf", tag="neg_max1")
         for n in range(PIECES):
             nc.scalar.activation(vals_bf[:, n * span : (n + 1) * span], pieces[n][:], ACT.Copy)
-        got2 = sbuf([P, I // 2], F32, "got_vals2")
-        nc.scalar.activation(got2[:].bitcast(BF16), vals_bf[:].indirect(offsets[:]), ACT.Copy)
+        got2 = sbuf([P, PAIRS], F32, "got_vals2")
+        nc.scalar.activation(got2[:].bitcast(BF16), listed(vals_bf, 0, I), ACT.Copy)
 
-        got3 = sbuf([P, I // 2], F32, "got_vals3")
-        nc.vector.tensor_copy(got3[:].bitcast(BF16), pools[3][:].indirect(offsets[:]))
+        got3 = sbuf([P, PAIRS], F32, "got_vals3")
+        nc.vector.tensor_copy(got3[:].bitcast(BF16), listed(pools[3], 0, I))
 
         v_bf = sbuf([P, BLOCKS * I], BF16, "v_bf", tag="neg_max1")
-        turn_values(got1[:], v_bf[:, I : 2 * I], "score0")
-        turn_values(got0[:], v_bf[:, :I], "bank5")
-        turn_values(got2[:], v_bf[:, 2 * I : 3 * I], "bank6")
-        turn_values(got3[:], v_bf[:, 3 * I :], "score1")
+        for block, got, number in ((1, got1, 0), (0, got0, 6), (2, got2, 2), (3, got3, 1)):
+            v_turned = bank(number, [P, 2, P], "v_turned")
+            for u in range(2):
+                nc.tensor.transpose(v_turned[:, u, :], got[:, u:PAIRS:2], ident[:])
+            nc.scalar.copy(
+                v_bf[:, block * I : (block + 1) * I].bitcast(F32).rearrange("p (e u) -> p e u", u=2),
+                v_turned[:].rearrange("p u e -> p e u"),
+            )
 
-        codes = sbuf([P, P + E], U32, "codes", tag="vals3")
-        scales = sbuf([P, P + E], U8, "scales")
+        codes = sbuf([P, E + P], U32, "codes", tag="vals3")
+        scales = sbuf([P, E + P], U8, "scales")
         early_codes = sbuf([P, P], U32, "early_codes")
         early_scales = sbuf([P, P], U8, "early_scales")
-        w_codes, w_scales = (codes[:, E:], early_codes[:]), (scales[:, E:], early_scales[:])
+        early, late = HALF_ORDER
+        w_codes = {early: early_codes[:], late: codes[:, E:]}
+        w_scales = {early: early_scales[:], late: scales[:, E:]}
 
         def quantize_weights(h):
             nc.vector.quantize_mx(w_codes[h].bitcast(FP8X4), w_scales[h], w_bf[:, h].rearrange("p q t -> p (q t)"))
 
-        def quantize_values(lo, hi):
-            v_codes, v_scales = codes[:, lo:hi], scales[:, lo:hi]
-            nc.vector.quantize_mx(v_codes.bitcast(FP8X4), v_scales, v_bf[:, PACK * lo : PACK * hi])
-            return v_codes, v_scales
-
-        out_rows = out.rearrange("(h p) e -> p h e", p=P)
-
-        def multiply(acc, h, operand):
-            v_codes, v_scales = operand
-            nc.tensor.matmul_mx(
-                acc, lhsT=w_codes[h].bitcast(FP8X4), lhsT_scale=w_scales[h],
-                rhs=v_codes.bitcast(FP8X4), rhs_scale=v_scales, start=True, stop=True,
+        def quantize_values(features):
+            nc.vector.quantize_mx(
+                codes[:, features].bitcast(FP8X4), scales[:, features],
+                v_bf[:, PACK * features.start : PACK * features.stop],
             )
 
-        quantize_weights(1)
-        first = quantize_values(0, 2 * P)
-        quantize_weights(0)
-        third = quantize_values(2 * P, 3 * P)
-        last = quantize_values(3 * P, E)
+        def multiply(acc, h, features):
+            nc.tensor.matmul_mx(
+                acc, lhsT=w_codes[h].bitcast(FP8X4), lhsT_scale=w_scales[h],
+                rhs=codes[:, features].bitcast(FP8X4), rhs_scale=scales[:, features], start=True, stop=True,
+            )
 
-        for h in (1, 0):
-            acc = psum.tile([P, 2 * P], F32, name="acc_first", tag=("bank7", "turned1")[h])
-            multiply(acc[:], h, first)
-            result = sbuf([P, 2 * P], F32, f"result_first{h}")
+        first_two, third, last = slice(0, 2 * P), slice(2 * P, 3 * P), slice(3 * P, E)
+        quantize_weights(early)
+        quantize_values(first_two)
+        quantize_weights(late)
+        quantize_values(third)
+        quantize_values(last)
+
+        out_rows = out.rearrange("(h p) e -> p h e", p=P)
+        for h in HALF_ORDER:
+            acc = bank((3, 5)[h], [P, 2 * P], "acc_first_two")
+            multiply(acc[:], h, first_two)
+            result = sbuf([P, 2 * P], F32, f"result_first_two{h}")
             nc.scalar.copy(result[:], acc[:])
-            nc.sync.dma_start(out_rows[:, h, : 2 * P], result[:])
+            nc.sync.dma_start(out_rows[:, h, first_two], result[:])
 
-        for block, operand, bank in ((2, third, "bank5"), (3, last, "turned0")):
-            acc = psum.tile([P, HALVES, P], F32, name="acc", tag=bank)
+        for name, features, number in (("third", third, 6), ("last", last, 7)):
+            acc = bank(number, [P, HALVES, P], f"acc_{name}")
             for h in range(HALVES):
-                multiply(acc[:, h, :], h, operand)
-            result = sbuf([P, HALVES, P], F32, f"result{block}")
+                multiply(acc[:, h, :], h, features)
+            result = sbuf([P, HALVES, P], F32, f"result_{name}")
             nc.vector.tensor_copy(result[:], acc[:])
-            nc.sync.dma_start(out_rows[:, :, block * P : (block + 1) * P], result[:])
+            nc.sync.dma_start(out_rows[:, :, features], result[:])

@@ -24,9 +24,6 @@ HALVES = Q // P
 BLOCKS = E // P
 PAIRS = I // 2
 APART = 8
-PIECES = 4
-EARLY_SLOTS = 128
-LARGEST_FACTOR = 2.0**126
 HALF_ORDER = (1, 0)
 
 
@@ -70,20 +67,10 @@ def tile_attend_sinkhorn_kernel(tc, query, keys_words, keys_scales, fac, vals, o
             nc.sync.dma_start(pool[:], vals[block * P : (block + 1) * P, :])
             return pool
 
-        span = T // PIECES
-
-        def load_piece(n):
-            piece = sbuf([P, span], F32, f"piece{n}")
-            nc.sync.dma_start(piece[:], vals[2 * P : 3 * P, n * span : (n + 1) * span])
-            return piece
-
+        pools = [load_values(block) for block in range(BLOCKS - 1)]
         fac_sb = sbuf([P, PACK], F32, "fac_sb")
         nc.sync.dma_start(fac_sb[:], fac.rearrange("(p t) o -> p (t o)", t=PACK))
-        pools = {0: load_values(0)}
-        pieces = [load_piece(n) for n in range(PIECES // 2)]
-        pools[1] = load_values(1)
-        pieces.extend(load_piece(n) for n in range(PIECES // 2, PIECES))
-        pools[3] = load_values(3)
+        pools.append(load_values(BLOCKS - 1))
 
         ident = sbuf([P, P], F32, "ident")
         make_identity(nc, ident[:])
@@ -117,37 +104,41 @@ def tile_attend_sinkhorn_kernel(tc, query, keys_words, keys_scales, fac, vals, o
                 )
             scores.append(score)
 
-        got0 = sbuf([P, PAIRS], F32, "got_vals0")
-        got1 = sbuf([P, PAIRS], F32, "got_vals1")
-        behind_query = sbuf([P, 2 * APART], F32, "behind_query", tag="query_bf1")
+        gots = [sbuf([P, PAIRS], F32, f"got_vals{block}") for block in range(BLOCKS)]
+
+        def gather_values(block, first_slot, end_slot):
+            nc.vector.tensor_copy(
+                gots[block][:].bitcast(BF16)[:, first_slot:end_slot], listed(pools[block], first_slot, end_slot)
+            )
+
+        neg_maxes = [sbuf([P, 1], F32, f"neg_max{h}", tag=("query_bf1", "neg_max1")[h]) for h in range(HALVES)]
 
         expds, row_sums = [], []
         for h in range(HALVES):
-            neg_max = behind_query[:, 0:1] if h == 0 else sbuf([P, 1], F32, "neg_max1")[:]
-            nc.vector.tensor_reduce(neg_max, scores[h][:], AXIS_X, ALU.max, negate=True)
+            nc.vector.tensor_reduce(neg_maxes[h][:], scores[h][:], AXIS_X, ALU.max, negate=True)
             expd = sbuf([P, PACK, P], F32, f"expd{h}")
             column = PAIRS // 2 + APART * h
-            row_sum = got0[:, column : column + 1]
+            row_sum = gots[0][:, column : column + 1]
             nc.scalar.activation(
                 expd[:], scores[h][:].rearrange("p (s t) -> p t s", t=PACK), ACT.Exp,
-                bias=neg_max, accum_out=row_sum,
+                bias=neg_maxes[h][:], accum_out=row_sum,
             )
             expds.append(expd)
             row_sums.append(row_sum)
-        fac_inv_raw = behind_query[:, APART : APART + PACK]
-        nc.vector.reciprocal(fac_inv_raw, fac_sb[:])
-        fac_inv = sbuf([P, PACK], F32, "fac_inv")
-        nc.gpsimd.tensor_scalar(fac_inv[:], fac_inv_raw, LARGEST_FACTOR, -LARGEST_FACTOR, ALU.min, ALU.max)
 
         rows = []
         for h in range(HALVES):
-            row_inv = got1[:, APART * h : APART * h + 1]
-            nc.vector.reciprocal(row_inv, row_sums[h])
+            row_inv = sbuf([P, 1], F32, f"row_inv{h}")
+            nc.vector.reciprocal(row_inv[:], row_sums[h])
             row = sbuf([P, PACK, P], F32, f"row{h}")
-            nc.vector.tensor_scalar(row[:], expds[h][:], row_inv, None, ALU.mult)
+            nc.scalar.activation(row[:], expds[h][:], ACT.Copy, scale=row_inv[:])
             rows.append(row)
 
-        both = [bank((2, 3, 4, 0)[t], [P, P], f"both{t}") for t in range(PACK)]
+        gather_values(0, 0, I // 2)
+        gather_values(0, I // 2, I)
+        gather_values(1, 0, I)
+
+        both = [bank(2 + t, [P, P], f"both{t}") for t in range(PACK)]
         for h in range(HALVES):
             for t in range(PACK):
                 nc.tensor.matmul(
@@ -155,24 +146,23 @@ def tile_attend_sinkhorn_kernel(tc, query, keys_words, keys_scales, fac, vals, o
                     start=(h == 0), stop=(h == HALVES - 1),
                 )
 
-        scaled = sbuf([P, PACK, P], BF16, "scaled")
+        summed = sbuf([P, PACK, P], BF16, "summed")
         col_sum = sbuf([P, PACK], F32, "col_sum")
         for t in range(PACK):
-            nc.scalar.activation(
-                scaled[:, t, :], both[t][:], ACT.Copy, scale=fac_inv[:, t : t + 1], accum_out=col_sum[:, t : t + 1]
-            )
+            nc.scalar.activation(summed[:, t, :], both[t][:], ACT.Copy, accum_out=col_sum[:, t : t + 1])
 
-        turned = [bank((2, 5)[h], [P, PACK, P], f"turned{h}") for h in range(HALVES)]
+        turned = [bank((2, 6)[h], [P, PACK, P], f"turned{h}") for h in range(HALVES)]
         for h in HALF_ORDER:
             for t in range(PACK):
                 nc.tensor.transpose(turned[h][:, t, :], rows[h][:, t, :], ident[:])
 
-        for first_slot, end_slot in ((0, EARLY_SLOTS), (EARLY_SLOTS, I)):
-            nc.vector.tensor_copy(got0[:].bitcast(BF16)[:, first_slot:end_slot], listed(pools[0], first_slot, end_slot))
-        nc.vector.tensor_copy(got1[:].bitcast(BF16), listed(pools[1], 0, I))
+        col_inv = sbuf([P, PACK], F32, "col_inv", tag="vals1")
+        nc.vector.reciprocal(col_inv[:], col_sum[:])
+        gain = sbuf([P, PACK], F32, "gain")
+        for t in range(PACK):
+            nc.scalar.activation(gain[:, t : t + 1], col_inv[:, t : t + 1], ACT.Copy, scale=fac_sb[:, t : t + 1])
 
-        gain = sbuf([P, PACK], F32, "gain", tag="vals1")
-        nc.vector.reciprocal(gain[:], col_sum[:])
+        gather_values(2, 0, I)
 
         w_bf = sbuf([P, HALVES, P, PACK], BF16, "w_bf")
         for h in HALF_ORDER:
@@ -181,35 +171,20 @@ def tile_attend_sinkhorn_kernel(tc, query, keys_words, keys_scales, fac, vals, o
                 gain[:].unsqueeze(1).to_broadcast([P, P, PACK]), ALU.mult,
             )
 
-        vals_bf = sbuf([P, T], BF16, "vals_bf", tag="neg_max1")
-        for n in range(PIECES):
-            nc.scalar.activation(vals_bf[:, n * span : (n + 1) * span], pieces[n][:], ACT.Copy)
-        got2 = sbuf([P, PAIRS], F32, "got_vals2")
-        nc.scalar.activation(got2[:].bitcast(BF16), listed(vals_bf, 0, I), ACT.Copy)
+        gather_values(3, 0, I)
 
-        got3 = sbuf([P, PAIRS], F32, "got_vals3")
-        nc.vector.tensor_copy(got3[:].bitcast(BF16), listed(pools[3], 0, I))
-
-        v_bf = sbuf([P, BLOCKS * I], BF16, "v_bf", tag="neg_max1")
-        for block, got, number in ((1, got1, 0), (0, got0, 6), (2, got2, 2), (3, got3, 1)):
-            v_turned = bank(number, [P, 2, P], "v_turned")
+        v_bf = sbuf([P, BLOCKS * I], BF16, "v_bf", tag="fac_sb")
+        for block in range(BLOCKS):
+            v_turned = bank((3, 4, 5, 7)[block], [P, 2, P], "v_turned")
             for u in range(2):
-                nc.tensor.transpose(v_turned[:, u, :], got[:, u:PAIRS:2], ident[:])
+                nc.tensor.transpose(v_turned[:, u, :], gots[block][:, u:PAIRS:2], ident[:])
             nc.scalar.copy(
                 v_bf[:, block * I : (block + 1) * I].bitcast(F32).rearrange("p (e u) -> p e u", u=2),
                 v_turned[:].rearrange("p u e -> p e u"),
             )
 
-        codes = sbuf([P, E + P], U32, "codes", tag="vals3")
-        scales = sbuf([P, E + P], U8, "scales")
-        early_codes = sbuf([P, P], U32, "early_codes")
-        early_scales = sbuf([P, P], U8, "early_scales")
-        early, late = HALF_ORDER
-        w_codes = {early: early_codes[:], late: codes[:, E:]}
-        w_scales = {early: early_scales[:], late: scales[:, E:]}
-
-        def quantize_weights(h):
-            nc.vector.quantize_mx(w_codes[h].bitcast(FP8X4), w_scales[h], w_bf[:, h].rearrange("p q t -> p (q t)"))
+        codes = sbuf([P, E + Q], U32, "codes", tag="vals3")
+        scales = sbuf([P, E + Q], U8, "scales")
 
         def quantize_values(features):
             nc.vector.quantize_mx(
@@ -218,27 +193,27 @@ def tile_attend_sinkhorn_kernel(tc, query, keys_words, keys_scales, fac, vals, o
             )
 
         def multiply(acc, h, features):
+            weights = slice(E + h * P, E + (h + 1) * P)
             nc.tensor.matmul_mx(
-                acc, lhsT=w_codes[h].bitcast(FP8X4), lhsT_scale=w_scales[h],
+                acc, lhsT=codes[:, weights].bitcast(FP8X4), lhsT_scale=scales[:, weights],
                 rhs=codes[:, features].bitcast(FP8X4), rhs_scale=scales[:, features], start=True, stop=True,
             )
 
         first_two, third, last = slice(0, 2 * P), slice(2 * P, 3 * P), slice(3 * P, E)
-        quantize_weights(early)
+        nc.vector.quantize_mx(codes[:, E:].bitcast(FP8X4), scales[:, E:], w_bf[:].rearrange("p h q t -> p (h q t)"))
         quantize_values(first_two)
-        quantize_weights(late)
         quantize_values(third)
         quantize_values(last)
 
         out_rows = out.rearrange("(h p) e -> p h e", p=P)
         for h in HALF_ORDER:
-            acc = bank((3, 5)[h], [P, 2 * P], "acc_first_two")
+            acc = bank(h, [P, 2 * P], "acc_first_two")
             multiply(acc[:], h, first_two)
             result = sbuf([P, 2 * P], F32, f"result_first_two{h}")
             nc.scalar.copy(result[:], acc[:])
             nc.sync.dma_start(out_rows[:, h, first_two], result[:])
 
-        for name, features, number in (("third", third, 6), ("last", last, 7)):
+        for name, features, number in (("third", third, 6), ("last", last, 2)):
             acc = bank(number, [P, HALVES, P], f"acc_{name}")
             for h in range(HALVES):
                 multiply(acc[:, h, :], h, features)

@@ -165,11 +165,18 @@ def tile_attend_sinkhorn_kernel(tc, query, keys_words, keys_scales, fac, vals, o
         gather_values(2, 0, I)
 
         w_bf = sbuf([P, HALVES, P, PACK], BF16, "w_bf")
-        for h in HALF_ORDER:
-            nc.vector.tensor_tensor(
-                w_bf[:, h], turned[h][:].rearrange("p t q -> p q t"),
-                gain[:].unsqueeze(1).to_broadcast([P, P, PACK]), ALU.mult,
-            )
+        on_vector, on_scalar = HALF_ORDER
+        nc.vector.tensor_tensor(
+            w_bf[:, on_vector], turned[on_vector][:].rearrange("p t q -> p q t"),
+            gain[:].unsqueeze(1).to_broadcast([P, P, PACK]), ALU.mult,
+        )
+        w_apart = sbuf([P, PACK, P], BF16, "w_apart")
+        for t in range(PACK):
+            nc.scalar.activation(w_apart[:, t, :], turned[on_scalar][:, t, :], ACT.Copy, scale=gain[:, t : t + 1])
+        nc.scalar.copy(
+            w_bf[:, on_scalar].rearrange("p (c i) t -> p c t i", i=4),
+            w_apart[:].rearrange("p t (c i) -> p c t i", i=4),
+        )
 
         gather_values(3, 0, I)
 
@@ -186,6 +193,12 @@ def tile_attend_sinkhorn_kernel(tc, query, keys_words, keys_scales, fac, vals, o
         codes = sbuf([P, E + Q], U32, "codes", tag="vals3")
         scales = sbuf([P, E + Q], U8, "scales")
 
+        def quantize_weights(h):
+            weights = slice(E + h * P, E + (h + 1) * P)
+            nc.vector.quantize_mx(
+                codes[:, weights].bitcast(FP8X4), scales[:, weights], w_bf[:, h].rearrange("p q t -> p (q t)")
+            )
+
         def quantize_values(features):
             nc.vector.quantize_mx(
                 codes[:, features].bitcast(FP8X4), scales[:, features],
@@ -200,8 +213,9 @@ def tile_attend_sinkhorn_kernel(tc, query, keys_words, keys_scales, fac, vals, o
             )
 
         first_two, third, last = slice(0, 2 * P), slice(2 * P, 3 * P), slice(3 * P, E)
-        nc.vector.quantize_mx(codes[:, E:].bitcast(FP8X4), scales[:, E:], w_bf[:].rearrange("p h q t -> p (h q t)"))
+        quantize_weights(on_vector)
         quantize_values(first_two)
+        quantize_weights(on_scalar)
         quantize_values(third)
         quantize_values(last)
 
@@ -213,10 +227,16 @@ def tile_attend_sinkhorn_kernel(tc, query, keys_words, keys_scales, fac, vals, o
             nc.scalar.copy(result[:], acc[:])
             nc.sync.dma_start(out_rows[:, h, first_two], result[:])
 
-        for name, features, number in (("third", third, 6), ("last", last, 2)):
-            acc = bank(number, [P, HALVES, P], f"acc_{name}")
-            for h in range(HALVES):
-                multiply(acc[:, h, :], h, features)
-            result = sbuf([P, HALVES, P], F32, f"result_{name}")
-            nc.vector.tensor_copy(result[:], acc[:])
-            nc.sync.dma_start(out_rows[:, :, features], result[:])
+        acc = bank(6, [P, HALVES, P], "acc_third")
+        for h in range(HALVES):
+            multiply(acc[:, h, :], h, third)
+        result = sbuf([P, HALVES, P], F32, "result_third")
+        nc.vector.tensor_copy(result[:], acc[:])
+        nc.sync.dma_start(out_rows[:, :, third], result[:])
+
+        for h, copy in enumerate((nc.scalar.copy, nc.vector.tensor_copy)):
+            acc = bank(2 + h, [P, P], "acc_last")
+            multiply(acc[:], h, last)
+            result = sbuf([P, P], F32, f"result_last{h}")
+            copy(result[:], acc[:])
+            nc.sync.dma_start(out_rows[:, h, last], result[:])

@@ -24,7 +24,7 @@ HALVES = Q // P
 BLOCKS = E // P
 PAIRS = I // 2
 APART = 8
-HALF_ORDER = (1, 0)
+LARGEST_FACTOR = 2.0**126
 
 
 def tile_attend_sinkhorn_kernel(tc, query, keys_words, keys_scales, fac, vals, offs, out):
@@ -67,10 +67,9 @@ def tile_attend_sinkhorn_kernel(tc, query, keys_words, keys_scales, fac, vals, o
             nc.sync.dma_start(pool[:], vals[block * P : (block + 1) * P, :])
             return pool
 
-        pools = [load_values(block) for block in range(BLOCKS - 1)]
         fac_sb = sbuf([P, PACK], F32, "fac_sb")
         nc.sync.dma_start(fac_sb[:], fac.rearrange("(p t) o -> p (t o)", t=PACK))
-        pools.append(load_values(BLOCKS - 1))
+        pools = [load_values(block) for block in range(BLOCKS)]
 
         ident = sbuf([P, P], F32, "ident")
         make_identity(nc, ident[:])
@@ -126,6 +125,11 @@ def tile_attend_sinkhorn_kernel(tc, query, keys_words, keys_scales, fac, vals, o
             expds.append(expd)
             row_sums.append(row_sum)
 
+        fac_inv_raw = sbuf([P, PACK], F32, "fac_inv_raw", tag="key_words")
+        nc.vector.reciprocal(fac_inv_raw[:], fac_sb[:])
+        fac_inv = sbuf([P, PACK], F32, "fac_inv")
+        nc.gpsimd.tensor_scalar(fac_inv[:], fac_inv_raw[:], LARGEST_FACTOR, -LARGEST_FACTOR, ALU.min, ALU.max)
+
         rows = []
         for h in range(HALVES):
             row_inv = sbuf([P, 1], F32, f"row_inv{h}")
@@ -138,96 +142,94 @@ def tile_attend_sinkhorn_kernel(tc, query, keys_words, keys_scales, fac, vals, o
         gather_values(0, I // 2, I)
         gather_values(1, 0, I)
 
-        both = [bank(2 + t, [P, P], f"both{t}") for t in range(PACK)]
+        turned = [bank(t, [P, HALVES, P], f"turned{t}") for t in range(PACK)]
         for h in range(HALVES):
             for t in range(PACK):
-                nc.tensor.matmul(
-                    both[t][:], lhsT=rows[h][:, t, :], rhs=ident[:], is_transpose=True,
-                    start=(h == 0), stop=(h == HALVES - 1),
-                )
+                nc.tensor.transpose(turned[t][:, h, :], rows[h][:, t, :], ident[:])
 
-        summed = sbuf([P, PACK, P], BF16, "summed")
+        summed = sbuf([P, PACK, Q], BF16, "summed")
         col_sum = sbuf([P, PACK], F32, "col_sum")
         for t in range(PACK):
-            nc.scalar.activation(summed[:, t, :], both[t][:], ACT.Copy, accum_out=col_sum[:, t : t + 1])
+            nc.scalar.activation(
+                summed[:, t, :], turned[t][:].rearrange("p h q -> p (h q)"), ACT.Copy,
+                scale=fac_inv[:, t : t + 1], accum_out=col_sum[:, t : t + 1],
+            )
 
-        turned = [bank((2, 6)[h], [P, PACK, P], f"turned{h}") for h in range(HALVES)]
-        for h in HALF_ORDER:
-            for t in range(PACK):
-                nc.tensor.transpose(turned[h][:, t, :], rows[h][:, t, :], ident[:])
+        v_bf = sbuf([P, BLOCKS * I], BF16, "v_bf")
 
-        col_inv = sbuf([P, PACK], F32, "col_inv", tag="vals1")
-        nc.vector.reciprocal(col_inv[:], col_sum[:])
-        gain = sbuf([P, PACK], F32, "gain")
-        for t in range(PACK):
-            nc.scalar.activation(gain[:, t : t + 1], col_inv[:, t : t + 1], ACT.Copy, scale=fac_sb[:, t : t + 1])
+        def turn_values(number, blocks):
+            v_turned = bank(number, [P, len(blocks), 2, P], "v_turned")
+            for n in reversed(range(len(blocks))):
+                for u in range(2):
+                    nc.tensor.transpose(v_turned[:, n, u, :], gots[blocks[n]][:, u:PAIRS:2], ident[:])
+            return v_turned
 
+        def copy_values(blocks, v_turned):
+            nc.scalar.copy(
+                v_bf[:, blocks[0] * I : (blocks[-1] + 1) * I].bitcast(F32).rearrange("p (n e u) -> p n e u", e=P, u=2),
+                v_turned[:].rearrange("p n u e -> p n e u"),
+            )
+
+        first_turned = turn_values(4, (0, 1))
+
+        gain = sbuf([P, PACK], F32, "gain", tag="vals1")
+        nc.vector.reciprocal(gain[:], col_sum[:])
         gather_values(2, 0, I)
 
+        w_apart = sbuf([P, PACK, Q], BF16, "w_apart")
         w_bf = sbuf([P, HALVES, P, PACK], BF16, "w_bf")
-        on_vector, on_scalar = HALF_ORDER
-        nc.vector.tensor_tensor(
-            w_bf[:, on_vector], turned[on_vector][:].rearrange("p t q -> p q t"),
-            gain[:].unsqueeze(1).to_broadcast([P, P, PACK]), ALU.mult,
-        )
-        w_apart = sbuf([P, PACK, P], BF16, "w_apart")
         for t in range(PACK):
-            nc.scalar.activation(w_apart[:, t, :], turned[on_scalar][:, t, :], ACT.Copy, scale=gain[:, t : t + 1])
-        nc.scalar.copy(
-            w_bf[:, on_scalar].rearrange("p (c i) t -> p c t i", i=4),
-            w_apart[:].rearrange("p t (c i) -> p c t i", i=4),
-        )
+            nc.scalar.activation(
+                w_apart[:, t, :], turned[t][:].rearrange("p h q -> p (h q)"), ACT.Copy, scale=gain[:, t : t + 1]
+            )
+        copy_values((0, 1), first_turned)
+        for h in range(HALVES):
+            nc.scalar.copy(
+                w_bf[:, h].rearrange("p (c i) t -> p c t i", i=4),
+                w_apart[:, :, h * P : (h + 1) * P].rearrange("p t (c i) -> p c t i", i=4),
+            )
 
         gather_values(3, 0, I)
 
-        v_bf = sbuf([P, BLOCKS * I], BF16, "v_bf", tag="fac_sb")
-        for block in range(BLOCKS):
-            v_turned = bank((3, 4, 5, 7)[block], [P, 2, P], "v_turned")
-            for u in range(2):
-                nc.tensor.transpose(v_turned[:, u, :], gots[block][:, u:PAIRS:2], ident[:])
-            nc.scalar.copy(
-                v_bf[:, block * I : (block + 1) * I].bitcast(F32).rearrange("p (e u) -> p e u", u=2),
-                v_turned[:].rearrange("p u e -> p e u"),
-            )
+        for block in range(2, BLOCKS):
+            copy_values((block,), turn_values(3 + block, (block,)))
 
         codes = sbuf([P, E + Q], U32, "codes", tag="vals3")
         scales = sbuf([P, E + Q], U8, "scales")
+        first_two, third, last = slice(0, 2 * P), slice(2 * P, 3 * P), slice(3 * P, E)
+        values = {part.start: (codes[:, part].bitcast(FP8X4), scales[:, part]) for part in (first_two, third, last)}
+        weights = [
+            (codes[:, E + h * P : E + (h + 1) * P].bitcast(FP8X4), scales[:, E + h * P : E + (h + 1) * P])
+            for h in range(HALVES)
+        ]
 
         def quantize_weights(h):
-            weights = slice(E + h * P, E + (h + 1) * P)
-            nc.vector.quantize_mx(
-                codes[:, weights].bitcast(FP8X4), scales[:, weights], w_bf[:, h].rearrange("p q t -> p (q t)")
-            )
+            nc.vector.quantize_mx(*weights[h], w_bf[:, h].rearrange("p q t -> p (q t)"))
 
         def quantize_values(features):
-            nc.vector.quantize_mx(
-                codes[:, features].bitcast(FP8X4), scales[:, features],
-                v_bf[:, PACK * features.start : PACK * features.stop],
-            )
+            nc.vector.quantize_mx(*values[features.start], v_bf[:, PACK * features.start : PACK * features.stop])
 
         def multiply(acc, h, features):
-            weights = slice(E + h * P, E + (h + 1) * P)
             nc.tensor.matmul_mx(
-                acc, lhsT=codes[:, weights].bitcast(FP8X4), lhsT_scale=scales[:, weights],
-                rhs=codes[:, features].bitcast(FP8X4), rhs_scale=scales[:, features], start=True, stop=True,
+                acc, lhsT=weights[h][0], lhsT_scale=weights[h][1],
+                rhs=values[features.start][0], rhs_scale=values[features.start][1], start=True, stop=True,
             )
 
-        first_two, third, last = slice(0, 2 * P), slice(2 * P, 3 * P), slice(3 * P, E)
-        quantize_weights(on_vector)
         quantize_values(first_two)
-        quantize_weights(on_scalar)
+        for h in range(HALVES):
+            quantize_weights(h)
         quantize_values(third)
         quantize_values(last)
 
         out_rows = out.rearrange("(h p) e -> p h e", p=P)
-        for h in HALF_ORDER:
+        for h in range(HALVES):
             acc = bank(h, [P, 2 * P], "acc_first_two")
             multiply(acc[:], h, first_two)
             result = sbuf([P, 2 * P], F32, f"result_first_two{h}")
             nc.scalar.copy(result[:], acc[:])
             nc.sync.dma_start(out_rows[:, h, first_two], result[:])
 
-        acc = bank(6, [P, HALVES, P], "acc_third")
+        acc = bank(7, [P, HALVES, P], "acc_third")
         for h in range(HALVES):
             multiply(acc[:, h, :], h, third)
         result = sbuf([P, HALVES, P], F32, "result_third")

@@ -142,7 +142,8 @@ def tile_attend_sinkhorn_kernel(tc, query, keys_words, keys_scales, fac, vals, o
         gather_values(0, I // 2, I)
         gather_values(1, 0, I)
 
-        turned = [bank(t, [P, HALVES, P], f"turned{t}") for t in range(PACK)]
+        banks = [bank(t, [P, 2, HALVES, P], f"turned{t}") for t in range(PACK)]
+        turned = [banks[t][:, 0] for t in range(PACK)]
         for h in range(HALVES):
             for t in range(PACK):
                 nc.tensor.transpose(turned[t][:, h, :], rows[h][:, t, :], ident[:])
@@ -151,26 +152,26 @@ def tile_attend_sinkhorn_kernel(tc, query, keys_words, keys_scales, fac, vals, o
         col_sum = sbuf([P, PACK], F32, "col_sum")
         for t in range(PACK):
             nc.scalar.activation(
-                summed[:, t, :], turned[t][:].rearrange("p h q -> p (h q)"), ACT.Copy,
+                summed[:, t, :], turned[t].rearrange("p h q -> p (h q)"), ACT.Copy,
                 scale=fac_inv[:, t : t + 1], accum_out=col_sum[:, t : t + 1],
             )
 
         v_bf = sbuf([P, BLOCKS * I], BF16, "v_bf")
 
-        def turn_values(number, blocks):
-            v_turned = bank(number, [P, len(blocks), 2, P], "v_turned")
-            for n in reversed(range(len(blocks))):
-                for u in range(2):
-                    nc.tensor.transpose(v_turned[:, n, u, :], gots[blocks[n]][:, u:PAIRS:2], ident[:])
-            return v_turned
+        def turn_values(block, v_turned):
+            for u in range(2):
+                nc.tensor.transpose(v_turned[:, u, :], gots[block][:, u:PAIRS:2], ident[:])
 
-        def copy_values(blocks, v_turned):
+        def copy_values(block, v_turned):
             nc.scalar.copy(
-                v_bf[:, blocks[0] * I : (blocks[-1] + 1) * I].bitcast(F32).rearrange("p (n e u) -> p n e u", e=P, u=2),
-                v_turned[:].rearrange("p n u e -> p n e u"),
+                v_bf[:, block * I : (block + 1) * I].bitcast(F32).rearrange("p (e u) -> p e u", u=2),
+                v_turned.rearrange("p u e -> p e u"),
             )
 
-        first_turned = turn_values(4, (0, 1))
+        v_turned = [banks[0][:, 1]] + [bank(3 + block, [P, 2, P], "v_turned")[:] for block in range(1, BLOCKS)]
+        turn_values(0, v_turned[0])
+        copy_values(0, v_turned[0])
+        turn_values(1, v_turned[1])
 
         gain = sbuf([P, PACK], F32, "gain", tag="vals1")
         nc.vector.reciprocal(gain[:], col_sum[:])
@@ -180,9 +181,9 @@ def tile_attend_sinkhorn_kernel(tc, query, keys_words, keys_scales, fac, vals, o
         w_bf = sbuf([P, HALVES, P, PACK], BF16, "w_bf")
         for t in range(PACK):
             nc.scalar.activation(
-                w_apart[:, t, :], turned[t][:].rearrange("p h q -> p (h q)"), ACT.Copy, scale=gain[:, t : t + 1]
+                w_apart[:, t, :], turned[t].rearrange("p h q -> p (h q)"), ACT.Copy, scale=gain[:, t : t + 1]
             )
-        copy_values((0, 1), first_turned)
+        copy_values(1, v_turned[1])
         for h in range(HALVES):
             nc.scalar.copy(
                 w_bf[:, h].rearrange("p (c i) t -> p c t i", i=4),
@@ -192,53 +193,46 @@ def tile_attend_sinkhorn_kernel(tc, query, keys_words, keys_scales, fac, vals, o
         gather_values(3, 0, I)
 
         for block in range(2, BLOCKS):
-            copy_values((block,), turn_values(3 + block, (block,)))
+            turn_values(block, v_turned[block])
+            copy_values(block, v_turned[block])
 
         codes = sbuf([P, E + Q], U32, "codes", tag="vals3")
         scales = sbuf([P, E + Q], U8, "scales")
-        first_two, third, last = slice(0, 2 * P), slice(2 * P, 3 * P), slice(3 * P, E)
-        values = {part.start: (codes[:, part].bitcast(FP8X4), scales[:, part]) for part in (first_two, third, last)}
-        weights = [
-            (codes[:, E + h * P : E + (h + 1) * P].bitcast(FP8X4), scales[:, E + h * P : E + (h + 1) * P])
-            for h in range(HALVES)
-        ]
+
+        def operand(first_column, end_column):
+            return codes[:, first_column:end_column].bitcast(FP8X4), scales[:, first_column:end_column]
+
+        weights = [operand(E + h * P, E + (h + 1) * P) for h in range(HALVES)]
 
         def quantize_weights(h):
             nc.vector.quantize_mx(*weights[h], w_bf[:, h].rearrange("p q t -> p (q t)"))
 
-        def quantize_values(features):
-            nc.vector.quantize_mx(*values[features.start], v_bf[:, PACK * features.start : PACK * features.stop])
-
-        def multiply(acc, h, features):
-            nc.tensor.matmul_mx(
-                acc, lhsT=weights[h][0], lhsT_scale=weights[h][1],
-                rhs=values[features.start][0], rhs_scale=values[features.start][1], start=True, stop=True,
-            )
-
-        quantize_values(first_two)
-        for h in range(HALVES):
-            quantize_weights(h)
-        quantize_values(third)
-        quantize_values(last)
+        def quantize_values(block):
+            nc.vector.quantize_mx(*operand(block * P, (block + 1) * P), v_bf[:, block * I : (block + 1) * I])
 
         out_rows = out.rearrange("(h p) e -> p h e", p=P)
-        for h in range(HALVES):
-            acc = bank(h, [P, 2 * P], "acc_first_two")
-            multiply(acc[:], h, first_two)
-            result = sbuf([P, 2 * P], F32, f"result_first_two{h}")
-            nc.scalar.copy(result[:], acc[:])
-            nc.sync.dma_start(out_rows[:, h, first_two], result[:])
 
-        acc = bank(7, [P, HALVES, P], "acc_third")
-        for h in range(HALVES):
-            multiply(acc[:, h, :], h, third)
-        result = sbuf([P, HALVES, P], F32, "result_third")
-        nc.vector.tensor_copy(result[:], acc[:])
-        nc.sync.dma_start(out_rows[:, :, third], result[:])
-
-        for h, copy in enumerate((nc.scalar.copy, nc.vector.tensor_copy)):
-            acc = bank(2 + h, [P, P], "acc_last")
-            multiply(acc[:], h, last)
-            result = sbuf([P, P], F32, f"result_last{h}")
+        def finish(number, h, first_block, end_block, copy):
+            features = slice(first_block * P, end_block * P)
+            values, value_scales = operand(features.start, features.stop)
+            acc = bank(number, [P, features.stop - features.start], "acc")
+            nc.tensor.matmul_mx(
+                acc[:], lhsT=weights[h][0], lhsT_scale=weights[h][1], rhs=values, rhs_scale=value_scales,
+                start=True, stop=True,
+            )
+            result = sbuf([P, features.stop - features.start], F32, f"result{number}")
             copy(result[:], acc[:])
-            nc.sync.dma_start(out_rows[:, h, last], result[:])
+            nc.sync.dma_start(out_rows[:, h, features], result[:])
+
+        for n in range(HALVES):
+            quantize_weights(n)
+            quantize_values(n)
+        for block in range(HALVES, BLOCKS):
+            quantize_values(block)
+
+        finish(0, 0, 0, 1, nc.scalar.copy)
+        finish(1, 1, 0, 2, nc.scalar.copy)
+        finish(7, 0, 1, 3, nc.vector.tensor_copy)
+        finish(4, 1, 2, 3, nc.scalar.copy)
+        finish(2, 0, 3, 4, nc.scalar.copy)
+        finish(3, 1, 3, 4, nc.vector.tensor_copy)

@@ -24,6 +24,7 @@ HALVES = Q // P
 BLOCKS = E // P
 PAIRS = I // 2
 APART = 8
+EARLY_SLOTS = 128
 LARGEST_FACTOR = 2.0**126
 
 
@@ -116,7 +117,7 @@ def tile_attend_sinkhorn_kernel(tc, query, keys_words, keys_scales, fac, vals, o
         for h in range(HALVES):
             nc.vector.tensor_reduce(neg_maxes[h][:], scores[h][:], AXIS_X, ALU.max, negate=True)
             expd = sbuf([P, PACK, P], F32, f"expd{h}")
-            column = PAIRS // 2 + APART * h
+            column = EARLY_SLOTS // 2 + APART * h
             row_sum = gots[0][:, column : column + 1]
             nc.scalar.activation(
                 expd[:], scores[h][:].rearrange("p (s t) -> p t s", t=PACK), ACT.Exp,
@@ -135,11 +136,15 @@ def tile_attend_sinkhorn_kernel(tc, query, keys_words, keys_scales, fac, vals, o
             row_inv = sbuf([P, 1], F32, f"row_inv{h}")
             nc.vector.reciprocal(row_inv[:], row_sums[h])
             row = sbuf([P, PACK, P], F32, f"row{h}")
-            nc.scalar.activation(row[:], expds[h][:], ACT.Copy, scale=row_inv[:])
+            for part in (slice(0, PACK // 2), slice(PACK // 2, PACK)):
+                if h == 0:
+                    nc.vector.tensor_scalar(row[:, part], expds[h][:, part], row_inv[:], None, ALU.mult)
+                else:
+                    nc.scalar.activation(row[:, part], expds[h][:, part], ACT.Copy, scale=row_inv[:])
             rows.append(row)
 
-        gather_values(0, 0, I // 2)
-        gather_values(0, I // 2, I)
+        gather_values(0, 0, EARLY_SLOTS)
+        gather_values(0, EARLY_SLOTS, I)
         gather_values(1, 0, I)
 
         banks = [bank(t, [P, 2, HALVES, P], f"turned{t}") for t in range(PACK)]

@@ -107,9 +107,12 @@ def tile_attend_sinkhorn_kernel(tc, query, keys_words, keys_scales, fac, vals, o
         gots = [sbuf([P, PAIRS], F32, f"got_vals{block}") for block in range(BLOCKS)]
 
         def gather_values(block, first_slot, end_slot):
-            nc.vector.tensor_copy(
-                gots[block][:].bitcast(BF16)[:, first_slot:end_slot], listed(pools[block], first_slot, end_slot)
-            )
+            got = gots[block][:].bitcast(BF16)
+            if block == 0:
+                got = got[:, first_slot:end_slot]
+            else:
+                got = got.rearrange("p (u s e) -> p s u e", u=2, e=2)
+            nc.vector.tensor_copy(got, listed(pools[block], first_slot, end_slot))
 
         neg_maxes = [sbuf([P, 1], F32, f"neg_max{h}", tag=("query_bf1", "neg_max1")[h]) for h in range(HALVES)]
 
@@ -165,7 +168,8 @@ def tile_attend_sinkhorn_kernel(tc, query, keys_words, keys_scales, fac, vals, o
 
         def turn_values(block, v_turned):
             for u in range(2):
-                nc.tensor.transpose(v_turned[:, u, :], gots[block][:, u:PAIRS:2], ident[:])
+                words = slice(u, PAIRS, 2) if block == 0 else slice(u * P, (u + 1) * P)
+                nc.tensor.transpose(v_turned[:, u, :], gots[block][:, words], ident[:])
 
         def copy_values(block, v_turned):
             nc.scalar.copy(

@@ -208,8 +208,11 @@ def tile_attend_sinkhorn_kernel(tc, query, keys_words, keys_scales, fac, vals, o
         codes = sbuf([P, E + Q], U32, "codes", tag="vals3")
         scales = sbuf([P, E + Q], U8, "scales")
 
+        first_codes = sbuf([P, P], U32, "first_codes")
+
         def operand(first_column, end_column):
-            return codes[:, first_column:end_column].bitcast(FP8X4), scales[:, first_column:end_column]
+            words = first_codes[:] if first_column == 0 else codes[:, first_column:end_column]
+            return words.bitcast(FP8X4), scales[:, first_column:end_column]
 
         weights = [operand(E + h * P, E + (h + 1) * P) for h in range(HALVES)]
 
@@ -233,15 +236,15 @@ def tile_attend_sinkhorn_kernel(tc, query, keys_words, keys_scales, fac, vals, o
             copy(result[:], acc[:])
             nc.sync.dma_start(out_rows[:, h, features], result[:])
 
-        for n in range(HALVES):
-            quantize_weights(n)
-            quantize_values(n)
-        for block in range(HALVES, BLOCKS):
+        quantize_values(0)
+        for h in range(HALVES):
+            quantize_weights(h)
+        for block in range(1, BLOCKS):
             quantize_values(block)
 
         finish(0, 0, 0, 1, nc.scalar.copy)
-        finish(1, 1, 0, 2, nc.scalar.copy)
+        finish(1, 1, 0, 1, nc.scalar.copy)
         finish(7, 0, 1, 3, nc.vector.tensor_copy)
-        finish(4, 1, 2, 3, nc.scalar.copy)
-        finish(2, 0, 3, 4, nc.scalar.copy)
-        finish(3, 1, 3, 4, nc.vector.tensor_copy)
+        finish(4, 1, 1, 3, nc.scalar.copy)
+        finish(2, 0, 3, 4, nc.vector.tensor_copy)
+        finish(3, 1, 3, 4, nc.scalar.copy)

@@ -32,7 +32,11 @@ def tile_attend_sinkhorn_kernel(tc, query, keys_words, keys_scales, fac, vals, o
     nc = tc.nc
     with ExitStack() as ctx:
         keep = ctx.enter_context(tc.tile_pool(name="keep", bufs=1))
+        laid = ctx.enter_context(tc.tile_pool(name="laid", bufs=1))
         psum = ctx.enter_context(tc.psum_pool(name="psum", bufs=1))
+
+        def laid_at(first_byte, shape, dtype, name):
+            return laid.tile(shape, dtype, name=name, align_bytes=64, offset=first_byte)
 
         def sbuf(shape, dtype, name, tag=None):
             return keep.tile(shape, dtype, name=name, tag=tag or name, align_bytes=64)
@@ -64,7 +68,7 @@ def tile_attend_sinkhorn_kernel(tc, query, keys_words, keys_scales, fac, vals, o
         query_raw.append(load_query(1))
 
         def load_values(block):
-            pool = sbuf([P, T], F32, f"vals{block}")
+            pool = laid_at(4 * T * block, [P, T], F32, f"vals{block}")
             nc.sync.dma_start(pool[:], vals[block * P : (block + 1) * P, :])
             return pool
 
@@ -74,6 +78,8 @@ def tile_attend_sinkhorn_kernel(tc, query, keys_words, keys_scales, fac, vals, o
 
         ident = sbuf([P, P], F32, "ident")
         make_identity(nc, ident[:])
+        minus_one = sbuf([P, PACK // 2], F32, "minus_one")
+        nc.gpsimd.memset(minus_one[:], -1.0)
 
         def listed(window, first_slot, end_slot):
             return window[:].indirect(offsets[:, first_slot // LIST_ROWS : end_slot // LIST_ROWS])
@@ -164,16 +170,20 @@ def tile_attend_sinkhorn_kernel(tc, query, keys_words, keys_scales, fac, vals, o
                 scale=fac_inv[:, t : t + 1], accum_out=col_sum[:, t : t + 1],
             )
 
-        v_bf = sbuf([P, BLOCKS * I], BF16, "v_bf")
+        v_bf = [None] * BLOCKS
 
         def turn_values(block, v_turned):
             for u in range(2):
                 words = slice(u, PAIRS, 2) if block == 0 else slice(u * P, (u + 1) * P)
                 nc.tensor.transpose(v_turned[:, u, :], gots[block][:, words], ident[:])
 
-        def copy_values(block, v_turned):
-            nc.scalar.copy(
-                v_bf[:, block * I : (block + 1) * I].bitcast(F32).rearrange("p (e u) -> p e u", u=2),
+        def copy_values(block, v_turned, copy=nc.scalar.copy):
+            if block == 1:
+                v_bf[block] = laid_at(4 * T * 2, [P, I], BF16, "v_bf1")
+            else:
+                v_bf[block] = sbuf([P, I], BF16, f"v_bf{block}")
+            copy(
+                v_bf[block][:].bitcast(F32).rearrange("p (e u) -> p e u", u=2),
                 v_turned.rearrange("p u e -> p e u"),
             )
 
@@ -182,9 +192,11 @@ def tile_attend_sinkhorn_kernel(tc, query, keys_words, keys_scales, fac, vals, o
         copy_values(0, v_turned[0])
         turn_values(1, v_turned[1])
 
-        gain = sbuf([P, PACK], F32, "gain", tag="vals1")
-        nc.vector.reciprocal(gain[:], col_sum[:])
+        gain = sbuf([P, PACK], F32, "gain")
+        for part in (slice(0, PACK // 2), slice(PACK // 2, PACK)):
+            nc.gpsimd.tensor_tensor(gain[:, part], col_sum[:, part], minus_one[:], ALU.pow)
         gather_values(2, 0, I)
+        copy_values(1, v_turned[1], nc.vector.tensor_copy)
 
         w_apart = sbuf([P, PACK, Q], BF16, "w_apart")
         w_bf = sbuf([P, HALVES, P, PACK], BF16, "w_bf")
@@ -192,7 +204,6 @@ def tile_attend_sinkhorn_kernel(tc, query, keys_words, keys_scales, fac, vals, o
             nc.scalar.activation(
                 w_apart[:, t, :], turned[t].rearrange("p h q -> p (h q)"), ACT.Copy, scale=gain[:, t : t + 1]
             )
-        copy_values(1, v_turned[1])
         for h in range(HALVES):
             nc.scalar.copy(
                 w_bf[:, h].rearrange("p (c i) t -> p c t i", i=4),
@@ -205,10 +216,10 @@ def tile_attend_sinkhorn_kernel(tc, query, keys_words, keys_scales, fac, vals, o
             turn_values(block, v_turned[block])
             copy_values(block, v_turned[block])
 
-        codes = sbuf([P, E + Q], U32, "codes", tag="vals3")
+        codes = laid_at(4 * T * 3, [P, E + Q], U32, "codes")
         scales = sbuf([P, E + Q], U8, "scales")
 
-        first_codes = sbuf([P, P], U32, "first_codes")
+        first_codes = laid_at(4 * T * 2 + 2 * I, [P, P], U32, "first_codes")
 
         def operand(first_column, end_column):
             words = first_codes[:] if first_column == 0 else codes[:, first_column:end_column]
@@ -220,7 +231,7 @@ def tile_attend_sinkhorn_kernel(tc, query, keys_words, keys_scales, fac, vals, o
             nc.vector.quantize_mx(*weights[h], w_bf[:, h].rearrange("p q t -> p (q t)"))
 
         def quantize_values(block):
-            nc.vector.quantize_mx(*operand(block * P, (block + 1) * P), v_bf[:, block * I : (block + 1) * I])
+            nc.vector.quantize_mx(*operand(block * P, (block + 1) * P), v_bf[block][:])
 
         out_rows = out.rearrange("(h p) e -> p h e", p=P)
 

@@ -212,9 +212,16 @@ def tile_attend_sinkhorn_kernel(tc, query, keys_words, keys_scales, fac, vals, o
 
         gather_values(3, 0, I)
 
-        for block in range(2, BLOCKS):
-            turn_values(block, v_turned[block])
-            copy_values(block, v_turned[block])
+        turn_values(2, v_turned[2])
+        copy_values(2, v_turned[2])
+        turn_values(3, v_turned[3])
+        last_parts = (slice(0, P // 2), slice(P // 2, P))
+        v_last = sbuf([P, P, PACK], BF16, "v_last")
+        for part in last_parts:
+            nc.scalar.copy(
+                v_last[:].rearrange("p e t -> p (e t)").bitcast(F32).rearrange("p (e u) -> p e u", u=2)[:, part],
+                v_turned[3].rearrange("p u e -> p e u")[:, part],
+            )
 
         codes = laid_at(4 * T * 3, [P, E + Q], U32, "codes")
         scales = sbuf([P, E + Q], U8, "scales")
@@ -250,8 +257,12 @@ def tile_attend_sinkhorn_kernel(tc, query, keys_words, keys_scales, fac, vals, o
         quantize_values(0)
         for h in range(HALVES):
             quantize_weights(h)
-        for block in range(1, BLOCKS):
+        for block in range(1, BLOCKS - 1):
             quantize_values(block)
+        for part in last_parts:
+            nc.vector.quantize_mx(
+                *operand(E - P + part.start, E - P + part.stop), v_last[:, part].rearrange("p e t -> p (e t)")
+            )
 
         finish(0, 0, 0, 1, nc.scalar.copy)
         finish(1, 1, 0, 1, nc.scalar.copy)

@@ -242,16 +242,19 @@ def tile_attend_sinkhorn_kernel(tc, query, keys_words, keys_scales, fac, vals, o
 
         out_rows = out.rearrange("(h p) e -> p h e", p=P)
 
-        def finish(number, h, first_block, end_block, copy):
-            features = slice(first_block * P, end_block * P)
+        def multiply(number, h, features, copy, result):
             values, value_scales = operand(features.start, features.stop)
             acc = bank(number, [P, features.stop - features.start], "acc")
             nc.tensor.matmul_mx(
                 acc[:], lhsT=weights[h][0], lhsT_scale=weights[h][1], rhs=values, rhs_scale=value_scales,
                 start=True, stop=True,
             )
+            copy(result, acc[:])
+
+        def finish(number, h, first_block, end_block, copy):
+            features = slice(first_block * P, end_block * P)
             result = sbuf([P, features.stop - features.start], F32, f"result{number}")
-            copy(result[:], acc[:])
+            multiply(number, h, features, copy, result[:])
             nc.sync.dma_start(out_rows[:, h, features], result[:])
 
         quantize_values(0)
@@ -268,5 +271,8 @@ def tile_attend_sinkhorn_kernel(tc, query, keys_words, keys_scales, fac, vals, o
         finish(1, 1, 0, 1, nc.scalar.copy)
         finish(7, 0, 1, 3, nc.vector.tensor_copy)
         finish(4, 1, 1, 3, nc.scalar.copy)
-        finish(2, 0, 3, 4, nc.vector.tensor_copy)
-        finish(3, 1, 3, 4, nc.scalar.copy)
+        last_features = slice(E - P, E)
+        last_result = sbuf([P, HALVES, P], F32, "last_result")
+        multiply(2, 0, last_features, nc.vector.tensor_copy, last_result[:, 0])
+        multiply(3, 1, last_features, nc.scalar.copy, last_result[:, 1])
+        nc.sync.dma_start(out_rows[:, :, last_features], last_result[:])

@@ -269,10 +269,10 @@ def tile_attend_sinkhorn_kernel(tc, query, keys_words, keys_scales, fac, vals, o
 
         finish(0, 0, 0, 1, nc.scalar.copy)
         finish(1, 1, 0, 1, nc.scalar.copy)
-        finish(7, 0, 1, 3, nc.vector.tensor_copy)
-        finish(4, 1, 1, 3, nc.scalar.copy)
-        last_features = slice(E - P, E)
-        last_result = sbuf([P, HALVES, P], F32, "last_result")
-        multiply(2, 0, last_features, nc.vector.tensor_copy, last_result[:, 0])
-        multiply(3, 1, last_features, nc.scalar.copy, last_result[:, 1])
-        nc.sync.dma_start(out_rows[:, :, last_features], last_result[:])
+        for h, numbers in enumerate(((2, 3), (7, 4))):
+            result = sbuf([P, 2, P], F32, f"middle{h}")
+            for n, copy in enumerate((nc.scalar.copy, nc.vector.tensor_copy)):
+                multiply(numbers[n], h, slice((1 + n) * P, (2 + n) * P), copy, result[:, n])
+            nc.sync.dma_start(out_rows[:, h, P : E - P], result[:].rearrange("p n e -> p (n e)"))
+        finish(5, 0, 3, 4, nc.scalar.copy)
+        finish(6, 1, 3, 4, nc.vector.tensor_copy)

@@ -23,9 +23,13 @@ LIST_ROWS = 16
 HALVES = Q // P
 BLOCKS = E // P
 PAIRS = I // 2
-APART = 8
-EARLY_SLOTS = 128
 LARGEST_FACTOR = 2.0**126
+VECTOR_SLOTS_LAST = I // 2
+
+POOL_BYTES = 4 * T
+PIECE_BYTES = 1024
+GAIN_AT = POOL_BYTES * BLOCKS
+LAST_POOL_AT = POOL_BYTES * (BLOCKS - 1)
 
 
 def tile_attend_sinkhorn_kernel(tc, query, keys_words, keys_scales, fac, vals, offs, out):
@@ -68,7 +72,7 @@ def tile_attend_sinkhorn_kernel(tc, query, keys_words, keys_scales, fac, vals, o
         query_raw.append(load_query(1))
 
         def load_values(block):
-            pool = laid_at(4 * T * block, [P, T], F32, f"vals{block}")
+            pool = laid_at(POOL_BYTES * block, [P, T], F32, f"vals{block}")
             nc.sync.dma_start(pool[:], vals[block * P : (block + 1) * P, :])
             return pool
 
@@ -78,8 +82,6 @@ def tile_attend_sinkhorn_kernel(tc, query, keys_words, keys_scales, fac, vals, o
 
         ident = sbuf([P, P], F32, "ident")
         make_identity(nc, ident[:])
-        minus_one = sbuf([P, PACK // 2], F32, "minus_one")
-        nc.gpsimd.memset(minus_one[:], -1.0)
 
         def listed(window, first_slot, end_slot):
             return window[:].indirect(offsets[:, first_slot // LIST_ROWS : end_slot // LIST_ROWS])
@@ -112,13 +114,16 @@ def tile_attend_sinkhorn_kernel(tc, query, keys_words, keys_scales, fac, vals, o
 
         gots = [sbuf([P, PAIRS], F32, f"got_vals{block}") for block in range(BLOCKS)]
 
-        def gather_values(block, first_slot, end_slot):
-            got = gots[block][:].bitcast(BF16)
-            if block == 0:
-                got = got[:, first_slot:end_slot]
-            else:
-                got = got.rearrange("p (u s e) -> p s u e", u=2, e=2)
-            nc.vector.tensor_copy(got, listed(pools[block], first_slot, end_slot))
+        def gather_on_vector(block, first_slot, end_slot):
+            nc.vector.tensor_copy(
+                gots[block][:].bitcast(BF16)[:, first_slot:end_slot], listed(pools[block], first_slot, end_slot)
+            )
+
+        def gather_on_scalar(block, first_slot, end_slot):
+            nc.scalar.activation(
+                gots[block][:].bitcast(BF16)[:, first_slot:end_slot], listed(pools[block], first_slot, end_slot),
+                ACT.Copy,
+            )
 
         neg_maxes = [sbuf([P, 1], F32, f"neg_max{h}", tag=("query_bf1", "neg_max1")[h]) for h in range(HALVES)]
 
@@ -126,11 +131,10 @@ def tile_attend_sinkhorn_kernel(tc, query, keys_words, keys_scales, fac, vals, o
         for h in range(HALVES):
             nc.vector.tensor_reduce(neg_maxes[h][:], scores[h][:], AXIS_X, ALU.max, negate=True)
             expd = sbuf([P, PACK, P], F32, f"expd{h}")
-            column = EARLY_SLOTS // 2 + APART * h
-            row_sum = gots[0][:, column : column + 1]
+            row_sum = sbuf([P, 1], F32, f"row_sum{h}")
             nc.scalar.activation(
                 expd[:], scores[h][:].rearrange("p (s t) -> p t s", t=PACK), ACT.Exp,
-                bias=neg_maxes[h][:], accum_out=row_sum,
+                bias=neg_maxes[h][:], accum_out=row_sum[:],
             )
             expds.append(expd)
             row_sums.append(row_sum)
@@ -140,139 +144,104 @@ def tile_attend_sinkhorn_kernel(tc, query, keys_words, keys_scales, fac, vals, o
         fac_inv = sbuf([P, PACK], F32, "fac_inv")
         nc.gpsimd.tensor_scalar(fac_inv[:], fac_inv_raw[:], LARGEST_FACTOR, -LARGEST_FACTOR, ALU.min, ALU.max)
 
+        added = [bank(t, [P, P], f"added{t}") for t in range(PACK)]
         rows = []
         for h in range(HALVES):
             row_inv = sbuf([P, 1], F32, f"row_inv{h}")
-            nc.vector.reciprocal(row_inv[:], row_sums[h])
+            nc.vector.reciprocal(row_inv[:], row_sums[h][:])
             row = sbuf([P, PACK, P], F32, f"row{h}")
             for part in (slice(0, PACK // 2), slice(PACK // 2, PACK)):
-                if h == 0:
-                    nc.vector.tensor_scalar(row[:, part], expds[h][:, part], row_inv[:], None, ALU.mult)
-                else:
-                    nc.scalar.activation(row[:, part], expds[h][:, part], ACT.Copy, scale=row_inv[:])
+                nc.vector.tensor_scalar(row[:, part], expds[h][:, part], row_inv[:], None, ALU.mult)
+            for t in range(PACK):
+                nc.tensor.matmul(
+                    added[t][:], lhsT=row[:, t, :], rhs=ident[:], is_transpose=True,
+                    start=h == 0, stop=h == HALVES - 1,
+                )
             rows.append(row)
 
-        gather_values(0, 0, EARLY_SLOTS)
-        gather_values(0, EARLY_SLOTS, I)
-        gather_values(1, 0, I)
-
-        banks = [bank(t, [P, 2, HALVES, P], f"turned{t}") for t in range(PACK)]
-        turned = [banks[t][:, 0] for t in range(PACK)]
-        for h in range(HALVES):
-            for t in range(PACK):
-                nc.tensor.transpose(turned[t][:, h, :], rows[h][:, t, :], ident[:])
-
-        summed = sbuf([P, PACK, Q], BF16, "summed")
+        summed = sbuf([P, PACK, P], BF16, "summed")
         col_sum = sbuf([P, PACK], F32, "col_sum")
         for t in range(PACK):
-            nc.scalar.activation(
-                summed[:, t, :], turned[t].rearrange("p h q -> p (h q)"), ACT.Copy,
-                scale=fac_inv[:, t : t + 1], accum_out=col_sum[:, t : t + 1],
+            nc.vector.tensor_scalar(
+                summed[:, t, :], added[t][:], fac_inv[:, t : t + 1], 0.0, ALU.mult, ALU.add,
+                accum_out=col_sum[:, t : t + 1],
             )
 
-        v_bf = [None] * BLOCKS
-
-        def turn_values(block, v_turned):
-            for u in range(2):
-                words = slice(u, PAIRS, 2) if block == 0 else slice(u * P, (u + 1) * P)
-                nc.tensor.transpose(v_turned[:, u, :], gots[block][:, words], ident[:])
-
-        def copy_values(block, v_turned, copy=nc.scalar.copy):
-            if block == 1:
-                v_bf[block] = laid_at(4 * T * 2, [P, I], BF16, "v_bf1")
-            else:
-                v_bf[block] = sbuf([P, I], BF16, f"v_bf{block}")
-            copy(
-                v_bf[block][:].bitcast(F32).rearrange("p (e u) -> p e u", u=2),
-                v_turned.rearrange("p u e -> p e u"),
-            )
-
-        v_turned = [banks[0][:, 1]] + [bank(3 + block, [P, 2, P], "v_turned")[:] for block in range(1, BLOCKS)]
-        turn_values(0, v_turned[0])
-        copy_values(0, v_turned[0])
-        turn_values(1, v_turned[1])
-
-        gain = sbuf([P, PACK], F32, "gain")
-        for part in (slice(0, PACK // 2), slice(PACK // 2, PACK)):
-            nc.gpsimd.tensor_tensor(gain[:, part], col_sum[:, part], minus_one[:], ALU.pow)
-        gather_values(2, 0, I)
-        copy_values(1, v_turned[1], nc.vector.tensor_copy)
-
-        w_apart = sbuf([P, PACK, Q], BF16, "w_apart")
-        w_bf = sbuf([P, HALVES, P, PACK], BF16, "w_bf")
-        for t in range(PACK):
-            nc.scalar.activation(
-                w_apart[:, t, :], turned[t].rearrange("p h q -> p (h q)"), ACT.Copy, scale=gain[:, t : t + 1]
-            )
+        turned = [bank(h, [P, PACK, P], f"turned{h}") for h in range(HALVES)]
         for h in range(HALVES):
-            nc.scalar.copy(
-                w_bf[:, h].rearrange("p (c i) t -> p c t i", i=4),
-                w_apart[:, :, h * P : (h + 1) * P].rearrange("p t (c i) -> p c t i", i=4),
+            for t in range(PACK):
+                nc.tensor.transpose(turned[h][:, t, :], rows[h][:, t, :], ident[:])
+        gain = laid_at(GAIN_AT, [P, PACK], F32, "gain")
+        nc.vector.reciprocal(gain[:], col_sum[:])
+
+        w_bf = sbuf([P, HALVES, P, PACK], BF16, "w_bf")
+        for h in range(HALVES):
+            nc.vector.tensor_tensor(
+                w_bf[:, h], turned[h][:].rearrange("p t q -> p q t"),
+                gain[:].unsqueeze(1).to_broadcast([P, P, PACK]), ALU.mult,
             )
 
-        gather_values(3, 0, I)
+        last = BLOCKS - 1
+        for block in range(last):
+            gather_on_scalar(block, 0, I)
+        gather_on_vector(last, 0, VECTOR_SLOTS_LAST)
+        gather_on_scalar(last, VECTOR_SLOTS_LAST, I)
 
-        turn_values(2, v_turned[2])
-        copy_values(2, v_turned[2])
-        turn_values(3, v_turned[3])
-        last_parts = (slice(0, P // 2), slice(P // 2, P))
-        v_last = sbuf([P, P, PACK], BF16, "v_last")
-        for part in last_parts:
-            nc.scalar.copy(
-                v_last[:].rearrange("p e t -> p (e t)").bitcast(F32).rearrange("p (e u) -> p e u", u=2)[:, part],
-                v_turned[3].rearrange("p u e -> p e u")[:, part],
-            )
-
-        codes = laid_at(4 * T * 3, [P, E + Q], U32, "codes")
+        first_codes = laid_at(GAIN_AT, [P, P], U32, "first_codes")
+        late_codes = laid_at(LAST_POOL_AT + 4 * PIECE_BYTES, [P, E], U32, "late_codes")
+        w_codes = sbuf([P, E + Q], U32, "w_codes")
         scales = sbuf([P, E + Q], U8, "scales")
 
-        first_codes = laid_at(4 * T * 2 + 2 * I, [P, P], U32, "first_codes")
-
         def operand(first_column, end_column):
-            words = first_codes[:] if first_column == 0 else codes[:, first_column:end_column]
-            return words.bitcast(FP8X4), scales[:, first_column:end_column]
+            words = first_codes if first_column < P else late_codes if first_column < E else w_codes
+            return words[:, first_column:end_column].bitcast(FP8X4), scales[:, first_column:end_column]
 
         weights = [operand(E + h * P, E + (h + 1) * P) for h in range(HALVES)]
-
-        def quantize_weights(h):
+        for h in range(HALVES):
             nc.vector.quantize_mx(*weights[h], w_bf[:, h].rearrange("p q t -> p (q t)"))
 
-        def quantize_values(block):
-            nc.vector.quantize_mx(*operand(block * P, (block + 1) * P), v_bf[block][:])
+        value_banks = (2, 3, 5, 6)
+
+        def prepare_values(block, v_bf, parts):
+            v_turned = bank(value_banks[block], [P, 2, P], f"v_turned{block}")
+            for u in range(2):
+                nc.tensor.transpose(v_turned[:, u, :], gots[block][:, u:PAIRS:2], ident[:])
+            words = v_bf[:].rearrange("p e t -> p (e t)").bitcast(F32).rearrange("p (e u) -> p e u", u=2)
+            for part in parts:
+                nc.scalar.copy(words[:, part], v_turned[:].rearrange("p u e -> p e u")[:, part])
+            for part in parts:
+                nc.vector.quantize_mx(
+                    *operand(block * P + part.start, block * P + part.stop),
+                    v_bf[:, part].rearrange("p e t -> p (e t)"),
+                )
+
+        places = (POOL_BYTES * 2, POOL_BYTES * 2 + PIECE_BYTES, LAST_POOL_AT)
+        for block in range(last):
+            v_bf = laid_at(places[block], [P, P, PACK], BF16, f"v_bf{block}")
+            prepare_values(block, v_bf, (slice(0, P),))
+        v_last = sbuf([P, P, PACK], BF16, "v_last")
+        prepare_values(last, v_last, (slice(0, P // 2), slice(P // 2, P)))
 
         out_rows = out.rearrange("(h p) e -> p h e", p=P)
 
-        def multiply(number, h, features, copy, result):
-            values, value_scales = operand(features.start, features.stop)
-            acc = bank(number, [P, features.stop - features.start], "acc")
+        def finish(number, h, block, copy, result):
+            values, value_scales = operand(block * P, (block + 1) * P)
+            acc = bank(number, [P, P], f"acc{number}")
             nc.tensor.matmul_mx(
                 acc[:], lhsT=weights[h][0], lhsT_scale=weights[h][1], rhs=values, rhs_scale=value_scales,
                 start=True, stop=True,
             )
-            copy(result, acc[:])
+            copy(result[:], acc[:])
+            nc.sync.dma_start(out_rows[:, h, block * P : (block + 1) * P], result[:])
 
-        def finish(number, h, first_block, end_block, copy):
-            features = slice(first_block * P, end_block * P)
-            result = sbuf([P, features.stop - features.start], F32, f"result{number}")
-            multiply(number, h, features, copy, result[:])
-            nc.sync.dma_start(out_rows[:, h, features], result[:])
-
-        quantize_values(0)
+        free_banks = (4, 7)
         for h in range(HALVES):
-            quantize_weights(h)
-        for block in range(1, BLOCKS - 1):
-            quantize_values(block)
-        for part in last_parts:
-            nc.vector.quantize_mx(
-                *operand(E - P + part.start, E - P + part.stop), v_last[:, part].rearrange("p e t -> p (e t)")
-            )
-
-        finish(0, 0, 0, 1, nc.scalar.copy)
-        finish(1, 1, 0, 1, nc.scalar.copy)
-        for h, numbers in enumerate(((2, 3), (7, 4))):
-            result = sbuf([P, 2, P], F32, f"middle{h}")
-            for n, copy in enumerate((nc.scalar.copy, nc.vector.tensor_copy)):
-                multiply(numbers[n], h, slice((1 + n) * P, (2 + n) * P), copy, result[:, n])
-            nc.sync.dma_start(out_rows[:, h, P : E - P], result[:].rearrange("p n e -> p (n e)"))
-        finish(5, 0, 3, 4, nc.scalar.copy)
-        finish(6, 1, 3, 4, nc.vector.tensor_copy)
+            result = laid_at(LAST_POOL_AT + PIECE_BYTES * (1 + h), [P, P], F32, f"first_result{h}")
+            finish(free_banks[h], h, 0, nc.vector.tensor_copy, result)
+        for block, banks, copy in ((1, value_banks, nc.scalar.copy), (2, free_banks, nc.vector.tensor_copy)):
+            for h in range(HALVES):
+                result = sbuf([P, P], F32, f"middle_result{block}{h}")
+                finish(banks[h], h, block, copy, result)
+        for h, copy in enumerate((nc.scalar.copy, nc.vector.tensor_copy)):
+            result = sbuf([P, P], F32, f"last_result{h}")
+            finish(h, h, last, copy, result)

from contextlib import ExitStack

import concourse.mybir as mybir
from concourse.masks import make_identity

D, T, I, Q, E = 512, 2048, 512, 256, 512
FLOPS = 2 * Q * D * I + 2 * Q * I * E

F32 = mybir.dt.float32
BF16 = mybir.dt.bfloat16
I32 = mybir.dt.int32
U32 = mybir.dt.uint32
U16 = mybir.dt.uint16
U8 = mybir.dt.uint8
FP8X4 = mybir.dt.float8_e4m3fn_x4
ALU = mybir.AluOpType
ACT = mybir.ActivationFunctionType
AXIS_X = mybir.AxisListType.X

P = 128
PACK = 4
LIST_ROWS = 16
HALVES = Q // P
BLOCKS = E // P
PAIRS = I // 2
LARGEST_FACTOR = 2.0**126
VECTOR_SLOTS_LAST = I // 2

POOL_BYTES = 4 * T
PIECE_BYTES = 1024
GAIN_AT = POOL_BYTES * BLOCKS
LAST_POOL_AT = POOL_BYTES * (BLOCKS - 1)


def tile_attend_sinkhorn_kernel(tc, query, keys_words, keys_scales, fac, vals, offs, out):
    nc = tc.nc
    with ExitStack() as ctx:
        keep = ctx.enter_context(tc.tile_pool(name="keep", bufs=1))
        laid = ctx.enter_context(tc.tile_pool(name="laid", bufs=1))
        psum = ctx.enter_context(tc.psum_pool(name="psum", bufs=1))

        def laid_at(first_byte, shape, dtype, name):
            return laid.tile(shape, dtype, name=name, align_bytes=64, offset=first_byte)

        def sbuf(shape, dtype, name, tag=None):
            return keep.tile(shape, dtype, name=name, tag=tag or name, align_bytes=64)

        def bank(number, shape, name):
            return psum.tile(shape, F32, name=name, tag=f"bank{number}")

        key_words = sbuf([P, T], U32, "key_words")
        words_rows = keys_words[0].rearrange("p n t -> p (n t)").bitcast(I32)
        nc.sync.dma_start(key_words[:, : T // 2].bitcast(I32), words_rows[:, : T // 2])

        offsets = keep.tile([P, I // LIST_ROWS], U16, name="offsets")
        nc.sync.dma_start(offsets[:], offs)

        key_scales = sbuf([P, T], U8, "key_scales")
        nc.gpsimd.memset(key_scales[:].bitcast(I32), 0)
        for r in range(4):
            nc.sync.dma_start(key_scales[r:P:32, :].bitcast(I32), keys_scales[0, r:16:4, :].bitcast(I32))

        query_rows = query.rearrange("(p j) q -> p j q", j=PACK)

        def load_query(h):
            raw = sbuf([P, PACK, P], F32, f"query_raw{h}")
            nc.sync.dma_start(raw[:], query_rows[:, :, h * P : (h + 1) * P])
            return raw

        query_raw = [load_query(0)]
        nc.sync.dma_start(key_words[:, T // 2 :].bitcast(I32), words_rows[:, T // 2 :])
        query_raw.append(load_query(1))

        def load_values(block):
            pool = laid_at(POOL_BYTES * block, [P, T], F32, f"vals{block}")
            nc.sync.dma_start(pool[:], vals[block * P : (block + 1) * P, :])
            return pool

        fac_sb = sbuf([P, PACK], F32, "fac_sb")
        nc.sync.dma_start(fac_sb[:], fac.rearrange("(p t) o -> p (t o)", t=PACK))
        pools = [load_values(block) for block in range(BLOCKS)]

        ident = sbuf([P, P], F32, "ident")
        make_identity(nc, ident[:])

        def listed(window, first_slot, end_slot):
            return window[:].indirect(offsets[:, first_slot // LIST_ROWS : end_slot // LIST_ROWS])

        got_scales = sbuf([P, I], U8, "got_scales")
        nc.vector.tensor_copy(got_scales[:], listed(key_scales, 0, I))

        slot_runs = (slice(0, I // 2), slice(I // 2, I))
        scores = []
        for h in range(HALVES):
            query_bf = sbuf([P, P, PACK], BF16, f"query_bf{h}")
            nc.scalar.copy(
                query_bf[:].rearrange("p (c i) j -> p c j i", i=4),
                query_raw[h][:].rearrange("p j (c i) -> p c j i", i=4),
            )
            q_codes = sbuf([P, P], U32, f"q_codes{h}")
            q_scales = sbuf([P, P], U8, f"q_scales{h}")
            nc.vector.quantize_mx(q_codes[:].bitcast(FP8X4), q_scales[:], query_bf[:].rearrange("p q j -> p (q j)"))
            if h == 0:
                got_words = sbuf([P, I], U32, "got_words", tag="query_bf0")
                for run in slot_runs:
                    nc.vector.tensor_copy(got_words[:, run], listed(key_words, run.start, run.stop))
            score = bank(h, [P, I], f"score{h}")
            for run in slot_runs:
                nc.tensor.matmul_mx(
                    score[:, run], lhsT=q_codes[:].bitcast(FP8X4), lhsT_scale=q_scales[:],
                    rhs=got_words[:, run].bitcast(FP8X4), rhs_scale=got_scales[:, run], start=True, stop=True,
                )
            scores.append(score)

        gots = [sbuf([P, PAIRS], F32, f"got_vals{block}") for block in range(BLOCKS)]

        def gather_on_vector(block, first_slot, end_slot):
            nc.vector.tensor_copy(
                gots[block][:].bitcast(BF16)[:, first_slot:end_slot], listed(pools[block], first_slot, end_slot)
            )

        def gather_on_scalar(block, first_slot, end_slot):
            nc.scalar.activation(
                gots[block][:].bitcast(BF16)[:, first_slot:end_slot], listed(pools[block], first_slot, end_slot),
                ACT.Copy,
            )

        neg_maxes = [sbuf([P, 1], F32, f"neg_max{h}", tag=("query_bf1", "neg_max1")[h]) for h in range(HALVES)]

        expds, row_sums = [], []
        for h in range(HALVES):
            nc.vector.tensor_reduce(neg_maxes[h][:], scores[h][:], AXIS_X, ALU.max, negate=True)
            expd = sbuf([P, PACK, P], F32, f"expd{h}")
            row_sum = sbuf([P, 1], F32, f"row_sum{h}")
            nc.scalar.activation(
                expd[:], scores[h][:].rearrange("p (s t) -> p t s", t=PACK), ACT.Exp,
                bias=neg_maxes[h][:], accum_out=row_sum[:],
            )
            expds.append(expd)
            row_sums.append(row_sum)

        fac_inv_raw = sbuf([P, PACK], F32, "fac_inv_raw", tag="key_words")
        nc.vector.reciprocal(fac_inv_raw[:], fac_sb[:])
        fac_inv = sbuf([P, PACK], F32, "fac_inv")
        nc.gpsimd.tensor_scalar(fac_inv[:], fac_inv_raw[:], LARGEST_FACTOR, -LARGEST_FACTOR, ALU.min, ALU.max)

        added = [bank(t, [P, P], f"added{t}") for t in range(PACK)]
        rows = []
        for h in range(HALVES):
            row_inv = sbuf([P, 1], F32, f"row_inv{h}")
            nc.vector.reciprocal(row_inv[:], row_sums[h][:])
            row = sbuf([P, PACK, P], F32, f"row{h}")
            for part in (slice(0, PACK // 2), slice(PACK // 2, PACK)):
                nc.vector.tensor_scalar(row[:, part], expds[h][:, part], row_inv[:], None, ALU.mult)
            for t in range(PACK):
                nc.tensor.matmul(
                    added[t][:], lhsT=row[:, t, :], rhs=ident[:], is_transpose=True,
                    start=h == 0, stop=h == HALVES - 1,
                )
            rows.append(row)

        summed = sbuf([P, PACK, P], BF16, "summed")
        col_sum = sbuf([P, PACK], F32, "col_sum")
        for t in range(PACK):
            nc.vector.tensor_scalar(
                summed[:, t, :], added[t][:], fac_inv[:, t : t + 1], 0.0, ALU.mult, ALU.add,
                accum_out=col_sum[:, t : t + 1],
            )

        turned = [bank(h, [P, PACK, P], f"turned{h}") for h in range(HALVES)]
        for h in range(HALVES):
            for t in range(PACK):
                nc.tensor.transpose(turned[h][:, t, :], rows[h][:, t, :], ident[:])
        gain = laid_at(GAIN_AT, [P, PACK], F32, "gain")
        nc.vector.reciprocal(gain[:], col_sum[:])

        w_bf = sbuf([P, HALVES, P, PACK], BF16, "w_bf")
        for h in range(HALVES):
            nc.vector.tensor_tensor(
                w_bf[:, h], turned[h][:].rearrange("p t q -> p q t"),
                gain[:].unsqueeze(1).to_broadcast([P, P, PACK]), ALU.mult,
            )

        last = BLOCKS - 1
        for block in range(last):
            gather_on_scalar(block, 0, I)
        gather_on_vector(last, 0, VECTOR_SLOTS_LAST)
        gather_on_scalar(last, VECTOR_SLOTS_LAST, I)

        first_codes = laid_at(GAIN_AT, [P, P], U32, "first_codes")
        late_codes = laid_at(LAST_POOL_AT + 4 * PIECE_BYTES, [P, E], U32, "late_codes")
        w_codes = sbuf([P, E + Q], U32, "w_codes")
        scales = sbuf([P, E + Q], U8, "scales")

        def operand(first_column, end_column):
            words = first_codes if first_column < P else late_codes if first_column < E else w_codes
            return words[:, first_column:end_column].bitcast(FP8X4), scales[:, first_column:end_column]

        weights = [operand(E + h * P, E + (h + 1) * P) for h in range(HALVES)]
        for h in range(HALVES):
            nc.vector.quantize_mx(*weights[h], w_bf[:, h].rearrange("p q t -> p (q t)"))

        value_banks = (2, 3, 5, 6)

        def prepare_values(block, v_bf, parts):
            v_turned = bank(value_banks[block], [P, 2, P], f"v_turned{block}")
            for u in range(2):
                nc.tensor.transpose(v_turned[:, u, :], gots[block][:, u:PAIRS:2], ident[:])
            words = v_bf[:].rearrange("p e t -> p (e t)").bitcast(F32).rearrange("p (e u) -> p e u", u=2)
            for part in parts:
                nc.scalar.copy(words[:, part], v_turned[:].rearrange("p u e -> p e u")[:, part])
            for part in parts:
                nc.vector.quantize_mx(
                    *operand(block * P + part.start, block * P + part.stop),
                    v_bf[:, part].rearrange("p e t -> p (e t)"),
                )

        places = (POOL_BYTES * 2, POOL_BYTES * 2 + PIECE_BYTES, LAST_POOL_AT)
        for block in range(last):
            v_bf = laid_at(places[block], [P, P, PACK], BF16, f"v_bf{block}")
            prepare_values(block, v_bf, (slice(0, P),))
        v_last = sbuf([P, P, PACK], BF16, "v_last")
        prepare_values(last, v_last, (slice(0, P // 2), slice(P // 2, P)))

        out_rows = out.rearrange("(h p) e -> p h e", p=P)

        def finish(number, h, block, copy, result):
            values, value_scales = operand(block * P, (block + 1) * P)
            acc = bank(number, [P, P], f"acc{number}")
            nc.tensor.matmul_mx(
                acc[:], lhsT=weights[h][0], lhsT_scale=weights[h][1], rhs=values, rhs_scale=value_scales,
                start=True, stop=True,
            )
            copy(result[:], acc[:])
            nc.sync.dma_start(out_rows[:, h, block * P : (block + 1) * P], result[:])

        free_banks = (4, 7)
        for h in range(HALVES):
            result = laid_at(LAST_POOL_AT + PIECE_BYTES * (1 + h), [P, P], F32, f"first_result{h}")
            finish(free_banks[h], h, 0, nc.vector.tensor_copy, result)
        for block, banks, copy in ((1, value_banks, nc.scalar.copy), (2, free_banks, nc.vector.tensor_copy)):
            for h in range(HALVES):
                result = sbuf([P, P], F32, f"middle_result{block}{h}")
                finish(banks[h], h, block, copy, result)
        for h, copy in enumerate((nc.scalar.copy, nc.vector.tensor_copy)):
            result = sbuf([P, P], F32, f"last_result{h}")
            finish(h, h, last, copy, result)
